import numpy as np, ml_dtypes
CORES = [25,29,65,69,153,157,193,197]
N = 8
BF = ml_dtypes.bfloat16
W, S, M, CAP, RO, DX = 4096, 1024, 12, 48, 3, 4
def places(g, w, k):
    u = np.add.reduce(w[..., :, None] * g, axis=-2) & 4095
    return ((u * u >> 5)[..., None, :] + k[..., :, None] * u[..., None, :]) & (W - 1)
def parts(rng):
    return (rng.integers(0, 256, (N, 8, 16, W), dtype=np.int32), rng.integers(0, 256, (N, 8, 16, S)), rng.integers(0, 256, (N, 8, 16, RO)),
            rng.integers(0, 3969, (N, 8, M)), rng.integers(620, 1000, (N, 8)))
def pack(x, g, w, k, t):
    return {"xs": x.reshape(N, 128, W).astype(np.float32).astype(BF), "gd": g.reshape(N, 128, S).astype(np.float32).astype(BF), "wt": w.reshape(N, 128, RO).astype(np.int32),
            "km": np.repeat(k, 16, axis=1).astype(np.int32), "th": np.repeat(t, 16, axis=1)[:, :, None].astype(np.int32)}
def plant(x, g, j, c, i, d):
    v = 255 - g[:, j]; n = np.arange(len(j)); a = v[i, n]
    v[i, n] = np.where(a < 128, a + d, a - d); x[:, c] = v
def lone(rng, x, g, w, k, s0, s1, lo, hi):
    c = places(g, w, k)[:, s0:s1]; m, j = np.nonzero((c >= lo) & (c < hi))
    if len(m):
        i = int(rng.integers(0, len(m))); x[:, c[m[i], j[i]]] = 255 - g[:, s0 + j[i]]
def setup_inputs(rng):
    x, g, w, k, t = parts(rng); h = rng.integers(0, 8)
    t[0, h] = 995; t[1, h] = 620; t[DX, h] = 620
    return pack(x, g, w, k, t)
def setup_inputs_room(rng):
    x, g, w, k, t = parts(rng); t = rng.integers(60, 129, (N, 8)); k = np.minimum(k | 1, 3967)
    for q in range(N):
        room = rng.permutation(np.array([0, 1, CAP - 1, CAP, CAP + 1, 2 * CAP, 0, CAP]))
        for h in range(8):
            c = places(g[q, h], w[q, h, :, 0], k[q, h])[rng.integers(0, M, S), np.arange(S)]
            o = rng.permutation(S); o = o[c[o] < W - 96]; first = np.unique(c[o], return_index=True)[1]
            o = o[np.sort(first)][:int(room[h])]; n = len(o)
            plant(x[q, h], g[q, h], o, c[o], rng.integers(0, 16, n), rng.integers(0, t[q, h], n))
    return pack(x, g, w, k, t)
def setup_inputs_ties(rng):
    x, g, w, k, t = parts(rng)
    w[:, :, 2, 0] = w[:, :, 1, 0]; g[:, :, 1] = np.minimum(g[:, :, 1], 254); g[:, :, 2] = np.maximum(g[:, :, 2], 1)
    for q in range(N):
        for h in (0, 2, 4, 6):
            n = int(rng.choice(np.array([CAP // 4, CAP // 2, CAP]))); t[q, h] = 3 if h == 2 * (q % 4) else rng.integers(1, 4)
            o = rng.permutation(S); a = np.minimum(o[:n], o[n:2 * n]); b = np.maximum(o[:n], o[n:2 * n]); e = o[2 * n:3 * n]
            kd = rng.integers(0, 4, n); kd[:4] = np.arange(4); s = (kd > 0).astype(np.int64)
            v = g[q, h][:, a].copy(); v[1] += s; v[2] -= s; g[q, h][:, b] = v
            c = places(g[q, h], w[q, h, :, 0], k[q, h])
            ca = c[rng.integers(0, M, n), a]; m = rng.integers(0, M, n); c1 = c[m, e]; c2 = c[(m + rng.integers(1, M, n)) % M, e]
            al = np.concatenate([ca, c1, c2]); one = np.bincount(al, minlength=W)[al] == 1
            pa = one[:n] & (ca < W - 96); pe = one[n:2 * n] & one[2 * n:]
            v = 255 - g[q, h][:, a]; v[1] -= ((kd == 1) | (kd == 2)).astype(np.int64); v[2] += (kd == 1).astype(np.int64); x[q, h][:, ca[pa]] = v[:, pa]
            i = rng.integers(0, 16, n); d = rng.integers(0, t[q, h], n)
            plant(x[q, h], g[q, h], e[pe], c1[pe], i[pe], d[pe]); plant(x[q, h], g[q, h], e[pe], c2[pe], i[pe], d[pe])
    a = int(rng.integers(0, S // 4)); b = a + int(rng.integers(1, S // 4))
    w[:, 1, :, 0] = 0; w[:, 1, 0, 0] = 1; k[:, 1, 0] = 0; k[:, 1, 1] = 3; t[:, 1] = 20
    g[:, 1, :, b] = g[:, 1, :, a].copy(); g[:, 1, 0, a] = 32; g[:, 1, 0, b] = 64
    x[:, 1, :, 128] = 255 - g[:, 1, :, a]; x[:, 1, 0, 128] = 207
    return pack(x, g, w, k, t)
def setup_inputs_ends(rng):
    x, g, w, k, t = parts(rng); o = rng.permutation(8); w[:, :, 0, 0] |= 1
    low = rng.integers(0, 192, (N, 4, W)); few = rng.integers(0, 64, (N, W)) == 0
    x[:, o[0], 0] = low[:, 0]; x[:, o[1], 0] = rng.integers(192, 256, (N, W))
    x[:, o[2], 0] = low[:, 1]; x[:, o[2], 0, 0] = 192; x[::2, o[2], 0, W - 1] = 255
    x[1::2, o[2], 0, W - 40] = 192; x[1::2, o[2], 0, W - 20] = 192
    x[:, o[3], 0, W // 2:] = low[:, 2, W // 2:]; x[:, o[4], 0] = np.where(few, 192, low[:, 3])
    x[:, o[6], 0, W - 81:] = low[:, 0, W - 81:]; x[:, o[7], 0, W - 81:] = low[:, 1, W - 81:]; x[:, o[7], 0, W - 4] = 192
    t[::2, o[0]] = 4080; t[1::2, o[0]] = 4; t[1::2, o[2]] = 4
    for q in range(1, N, 2):
        lone(rng, x[q, o[0]], g[q, o[0]], w[q, o[0], :, 0], k[q, o[0]], 0, S // 4, W // 2, W - 96)
        lone(rng, x[q, o[0]], g[q, o[0]], w[q, o[0], :, 1], k[q, o[0]], S // 4, S - 3 * CAP, 0, W // 4)
        lone(rng, x[q, o[2]], g[q, o[2]], w[q, o[2], :, 0], k[q, o[2]], 0, S, 0, W // 4)
    for q in range(N):
        for h in o[5:]:
            u = np.add.reduce(w[q, h, :, 0][:, None] * g[q, h], axis=0) & 4095; used = []
            for m, c in enumerate((W - 97, W - 96, 0)):
                for j in range(S):
                    if u[j] & 1 and j not in used:
                        v = int(u[j]); kk = (c - (v * v >> 5)) * pow(v, -1, W) % W
                        if kk <= 3968:
                            k[q, h, m] = kk; used.append(j)
                            plant(x[q, h], g[q, h], np.array([j]), np.array([c]), np.array([3 + m]), np.array([m])); break
    return pack(x, g, w, k, t)
def setup_inputs_alike(rng):
    x, g, w, k, t = parts(rng); o = rng.permutation(8)
    g[:, o[0]] = g[:, o[0], :, :1].copy()
    for q in range(N):
        c = places(g[q, o[0]], w[q, o[0], :, 0], k[q, o[0]])[:, 0]; m = np.flatnonzero(c < W - 96)[:1]
        plant(x[q, o[0]], g[q, o[0]], np.zeros(len(m), np.int64), c[m], m, np.full(len(m), 3))
    w[:, o[1]] = 0
    for q in range(N):
        e = np.arange(1, CAP + 1); d = np.append(e[::-1] if q % 2 == 0 else e, 0); n = np.arange(CAP + 1); i = rng.integers(0, 16, CAP + 1)
        v = np.repeat(255 - x[q, o[1], :, :1], CAP + 1, axis=1); a = v[i, n]
        v[i, n] = np.where(a < 128, a + d, a - d); g[q, o[1], :, :CAP + 1] = v
    k[:, o[2]] = k[:, o[2], :1].copy()
    g[:, o[3]] = g[:, o[3]][:, :, rng.integers(0, 4, S)]
    b = x[:, o[4], :, :8].copy(); b[:, 0, 0] = 200
    x[:, o[4]] = b[:, :, rng.integers(0, 8, W)]; g[:, o[4]] = 255 - b[:, :, rng.integers(0, 8, S)]
    k[:, o[5]] = rng.choice(np.array([0, 1, 3968]), (N, M))
    x[:, o[6]] = 255 * rng.integers(0, 2, (N, 16, W)); g[:, o[6]] = 255 * rng.integers(0, 2, (N, 16, S))
    w[:, o[7], :, 0] = 0; w[:, o[7], 0, 0] = 1; k[:, o[7]] = rng.integers(0, 8, (N, M)); t[:, o[7]] = 4080
    g[:, o[7], 0] = np.minimum(g[:, o[7], 0], 254); g[:, o[7], 0, S - 1] = 255
    for q in range(N):
        c = int(places(g[q, o[7]], w[q, o[7], :, 0], k[q, o[7]])[0, S - 1]); x[q, o[7], :, c] = 255 - g[q, o[7], :, S - 1]
    return pack(x, g, w, k, t)
def setup_inputs_spread(rng):
    x, g, w, k, t = parts(rng)
    def uneven(n):
        v = np.minimum((np.exp2(8 * rng.random((N, 8, 1, n))) * rng.random((N, 8, 16, n))).astype(np.int64), 255)
        return np.where(rng.random((N, 8, 1, n)) < 0.5, v, 255 - v)
    x = uneven(W); g = uneven(S)
    w = np.minimum(np.exp2(8 * rng.random(w.shape)).astype(np.int64), 255); k = np.minimum(np.exp2(12 * rng.random(k.shape)).astype(np.int64), 3968)
    t = np.minimum(np.maximum(np.exp2(12 * rng.random((N, 8))).astype(np.int64), 1), 4080); t[:, rng.integers(0, 8)] = rng.integers(1500, 2500, N)
    return pack(x, g, w, k, t)
def check_inputs(d):
    bad = []
    for n, lo, hi in (("xs", 0, 255), ("gd", 0, 255), ("wt", 0, 255), ("km", 0, 3968), ("th", 1, 4080)):
        a = np.asarray(d[n]).astype(np.float64)
        if not np.all((a >= lo) & (a <= hi) & (np.floor(a) == a)): bad.append("range of " + n)
    for n in ("km", "th"):
        a = np.asarray(d[n]).reshape(N, 8, 16, -1)
        if np.any(a != a[:, :, :1]): bad.append("rows of a group alike in " + n)
    return bad
def reference(xs, gd, wt, km, th):
    x = xs.astype(np.float32).astype(np.int32).reshape(N, 8, 16, W); g = gd.astype(np.float32).astype(np.int32).reshape(N, 8, 16, S)
    w = wt.astype(np.int64).reshape(N, 8, 16, RO); k = km.astype(np.int64).reshape(N, 8, 16, M)[:, :, 0]; t = th.astype(np.int64).reshape(N, 8, 16)[:, :, 0]
    log = np.zeros((N, 8, W), np.int64); place = np.arange(W); slot = np.arange(S); rows = np.arange(8)[:, None]
    for rnd in range(RO):
        cuts = []; gives = []; nx = []
        for a in range(N):
            c = places(g[a], w[a, :, :, rnd], k[a])
            v = np.take_along_axis(x[a], c.reshape(8, 1, M * S), 2).reshape(8, 16, M, S)
            D = np.add.reduce(np.abs(g[a][:, :, None, :] + v - 255), axis=1)
            m = np.argmin(D, axis=1)[:, None]
            D = np.take_along_axis(D, m, 1)[:, 0].astype(np.int64); c = np.take_along_axis(c, m, 1)[:, 0]
            fit = (D < t[a][:, None]) & (c < W - 96)
            cand = fit & (np.add.accumulate(fit.astype(np.int64), axis=1) <= CAP)
            key = D * S + slot; low = np.full((8, W), 2 ** 40, np.int64)
            np.minimum.at(low, (rows, c), np.where(cand, key, 2 ** 40))
            cut = cand & (np.take_along_axis(low, c, 1) == key)
            ok = (x[a][:, 0] >= 192) & (x[a][:, 0] <= 255)
            U = np.minimum.accumulate(np.where(ok, place, W - 1)[:, ::-1], axis=1)[:, ::-1]
            e1 = np.take_along_axis(U, np.minimum(c + 16, W - 1), 1); e2 = np.take_along_axis(U, np.minimum(e1 + 8, W - 1), 1)
            gives.append([np.maximum(255 - np.take_along_axis(x[a], e[:, None, :], 2), 0) for e in (np.minimum(c + 10, W - 1), e1, e2)])
            reach = np.full((8, W), -1, np.int64); np.maximum.at(reach, (rows, c), np.where(cut, e2, -1))
            gone = np.maximum.accumulate(reach, axis=1) >= place
            log[a] = np.where(gone & (log[a] == 0), rnd + 1, log[a])
            nx.append(np.where(gone[:, None, :], np.int32(512), x[a])); cuts.append(cut)
        ng = []
        for a in range(N):
            p, q = a ^ 1, a ^ DX
            every = np.concatenate([gives[p][0], gives[q][1], gives[q][2], g[a], g[a]], axis=2)
            there = np.concatenate([cuts[p], cuts[q], cuts[q], ~cuts[a], cuts[a]], axis=1)
            o = np.argsort(~there, axis=1, kind="stable")[:, :S]
            ng.append(np.take_along_axis(every, o[:, None, :], 2))
        x = np.stack(nx); g = np.stack(ng)
    return {"yg": g.reshape(N, 128, S).astype(np.float32).astype(BF), "yc": log.astype(np.float32)}

@@ -1,0 +1,537 @@
+from concourse.bass import DstId, RemoteDMATransfer
+from concourse.mybir import AluOpType as Op, AxisListType, ActivationFunctionType as Fn
+
+RO, M, S, W, CAP = 3, 12, 1024, 4096, 48
+POOLW = 192 + S + 240
+_F32 = """wf 3 KF 12 TH 1 KD 1 SW 3 Pf 1 PI 1 PG 1 P16 1 P256 1 BF 128 tA 128 tB 128 tC 128 WM 96 R48 48 RI 48 SLW 80 RBH 3 RC 3 PL 256
+ BM 16 EG 4 ZER 64 uf 64 Q 80 cur 192 fa 64 Cs 64 junk 192 sA 3 OH 48 M1 192 xk 48 US 144 tk 48 RV 48 vl 3 CKm 96 SLm 48 cw 3 kw 3 sw 3
+ tm 144 mn 3 eq 3 vv 3 nc 3 n5 3 pv 3 sel 48 T1 48 em 48 ew 6 UT 256 TU 256 fw 16 nf 1 wt4 1 CF 12 PO 4 ac 2 PF 12 lf 64
+ yct 768 CN 3 CNL 6"""
+_BF = """X 4096 GL 1024 YG 1024 Z 12288 A 12288 wb 3 Z1 144 Z64 144 Z128 144 ZN 144 ZW 432 B 128 NB 128 ID 128 NI 128 TN 128 TS 128 TQ 128
+ B0 128 TG 128 AG 128 IO 256 BI 768 C2 768 FB 64 CB 8 GX 144 GN 144 GV 144 LH 768 RH 1536 lc 1 R0 256 NK 256 tg 48 SND 1152 POOL 4368"""
+_I32 = """wi 3 ki 12 ti 1 IP 1 IPa 1 IPb 1 IQ 144 IQa 128 IQb 128 IZ 144 IJ 80 I256 256 WI 96 UW 80 FW 80 KW 80 u0 64 f0 64 CI 768 CM 768
+ fb 64 kI 48 mI 48 dm 48 ts 48 CK 96 p1 48 p1h 48 q1 3 q1l 3 CE 18 PJ 12"""
+_U16 = "CL 768 sO 4 DL 12 OFF 12 qO 4 LST 64 sl16 4"
+COLS, SCRATCH, PLACE = {}, {}, {}
+for _txt, _dt in ((_F32, "float32"), (_BF, "bfloat16"), (_I32, "int32"), (_U16, "uint16")):
+    _w, _at = _txt.split(), 16
+    for _k in range(0, len(_w), 2):
+        _n = int(_w[_k + 1])
+        COLS[_w[_k]] = _n
+        if _dt == "bfloat16" or _w[_k] in ("CN", "CNL"):
+            SCRATCH[_w[_k]] = ("sbuf", [128, _n], _dt)
+        else:
+            PLACE[_w[_k]] = ("all_" + _dt, _at)
+            _at += _n + (-_n) % 16
+    if _dt != "bfloat16":
+        SCRATCH["all_" + _dt] = ("sbuf", [128, _at], _dt)
+for _b in range(8):
+    SCRATCH["P%d" % _b] = ("psum", [128, 512], "float32")
+    COLS["P%d" % _b] = 512
+LOADS = ["dG", "dW", "dK", "dT", "dX", "dX2", "dR", "dM0", "dM1", "dY0", "dY1", "dC"]
+SEMAPHORES = ["sV", "sS", "sP", "sG", "lsem", "cn0", "cn1", "cn2", "ar0", "ar1", "ar2"] + LOADS
+
+SMS = (3, 9, 0, 6)
+RMS = (8, 10, 11)
+SCHED = """L1 SG3 L3 L2 VG11 L0 SG9 PX3 PX9 SA3 VR11 VG7 VG2 PK11 VG8 SG0 SA9 SG6 PX0 PK3 PK9 SA0 PX6 SV7 VG5 PK0 VR8 SV2 PK7 VG10 SV5
+ SA6 PK8 VG4 PK2 VR10 PK5 PK10 SV4 PK6 PK4 VG1 SV1 N0 PK1 N1""".split()
+
+
+def R(b, lo=0, hi=None):
+    return (b, lo, COLS[b] if hi is None else hi)
+
+
+def reg(x):
+    if not isinstance(x, str):
+        return x
+    p = x.split(":")
+    lo = int(p[1]) if len(p) > 1 else 0
+    return (p[0], lo, int(p[2]) if len(p) > 2 else lo + 1 if len(p) > 1 else COLS[p[0]])
+
+
+def sub(r, lo, hi):
+    return (r[0], r[1] + lo, r[1] + hi)
+
+
+def builder(g, T):
+    eng = {"V": g.vector, "S": g.scalar, "P": g.tensor, "G": g, "Y": g.sync}
+    cnt = {"V": 0, "S": 0, "P": 0, "G": 0}
+    know = {q: {} for q in eng}
+    snap = {}
+    hist = {}
+
+    def psum(b):
+        return b[0] == "P" and b[1:] in "01234567" and len(b) == 2
+
+    def wait(q, reads, writes):
+        want = {}
+        for regs, wr in ((reads, False), (writes, True)):
+            for b, lo, hi in regs:
+                ps = psum(b)
+                for h in hist.get(b, ()):
+                    same = h[3] == q
+                    if same and q == "P":
+                        continue
+                    over = h[0] < hi and lo < h[1]
+                    if ((ps and not same) or (over and (h[2] or wr))) and want.get(h[3], 0) < h[4]:
+                        want[h[3]] = h[4]
+        for e, c in sorted(want.items(), key=lambda x: (x[0] == q, x[0])):
+            k = know[q]
+            if k.get(e, 0) < c:
+                eng[q].wait_ge(T.sem["s" + e if e in cnt else e], c)
+                for e2, c2 in list(snap.get((e, c), {}).items()) + [(e, c)]:
+                    if k.get(e2, 0) < c2:
+                        k[e2] = c2
+
+    def log(reads, writes, e, c):
+        for regs, wr in ((reads, False), (writes, True)):
+            for b, lo, hi in regs:
+                h = hist.setdefault(b, [])
+                h[:] = [x for x in h if not (lo <= x[0] and x[1] <= hi and
+                                             ((x[3] == e and x[2] == wr) or (wr and not psum(b))))]
+                h.append([lo, hi, wr, e, c])
+
+    def op(q, call, reads, writes):
+        wait(q, reads, writes)
+        call().then_inc(T.sem["s" + q], 1)
+        cnt[q] += 1
+        snap[(q, cnt[q])] = dict(know[q])
+        log(reads, writes, q, cnt[q])
+
+    def dma(q, sem, out, in_, reads, writes):
+        wait(q, reads, writes)
+        eng[q].dma_start(out=out, in_=in_).then_inc(T.sem[sem], 16)
+        snap[(sem, 16)] = dict(know[q])
+        log(reads, writes, sem, 16)
+
+    def arrive(sem, val, writes):
+        log([], writes, sem, val)
+
+    return op, dma, arrive, wait, cnt
+
+
+def rank_program(g, core, T, topo):
+    rank = T.rank_of(core)
+    if rank is None:
+        return
+    op, dma, arrive, waits, cnt = builder(g, T)
+    V = g.vector
+
+    def v(r):
+        r = reg(r)
+        b, o = PLACE.get(r[0], (r[0], 0))
+        return T[b][:, o + r[1]:o + r[2]]
+
+    def back(b):
+        n, (b, o) = COLS[b], PLACE.get(b, (b, 0))
+        return T[b][:, o + n - 1:(o - 1 if o else None):-1]
+
+    def src(x, rd):
+        if isinstance(x, tuple) and len(x) == 2:
+            a, b = reg(x[0]), reg(x[1])
+            rd += [a, b]
+            return v(a).indirect(v(b))
+        if isinstance(x, (tuple, str)):
+            rd.append(reg(x))
+            return v(x)
+        return x
+
+    def tt(o, a, b, f):
+        rd = []
+        x, y = src(a, rd), src(b, rd)
+        op("V", lambda: V.tensor_tensor(out=v(o), in0=x, in1=y, op=f), rd, [reg(o)])
+
+    def ts(o, a, s1, f0, s2=None, f1=None):
+        rd = []
+        x, y, z = src(a, rd), src(s1, rd), src(s2, rd)
+        if f1 is None:
+            op("V", lambda: V.tensor_scalar(out=v(o), in0=x, scalar1=y, scalar2=None, op0=f0), rd, [reg(o)])
+        else:
+            op("V", lambda: V.tensor_scalar(out=v(o), in0=x, scalar1=y, scalar2=z, op0=f0, op1=f1), rd, [reg(o)])
+
+    def cp(o, a):
+        rd = []
+        x = src(a, rd)
+        op("V", lambda: V.tensor_copy(out=v(o), in_=x), rd, [reg(o)])
+
+    def scatter(win, lst, a):
+        op("V", lambda: V.tensor_copy(out=v(win).indirect(v(lst)), in_=v(a)), [reg(a), reg(lst)], [win])
+
+    def tr(o, a, f):
+        op("V", lambda: V.tensor_reduce(out=v(o), in_=v(a), axis=AxisListType.X, op=f), [reg(a)], [reg(o)])
+
+    def fill(o, x):
+        op("V", lambda: V.memset(v(o), x), [], [reg(o)])
+
+    def scan(o, a, b, ini, f0, f1, turn=False):
+        w = back if turn else v
+        op("V", lambda: V.tensor_tensor_scan(out=w(o), data0=w(a), data1=w(b), initial=ini, op0=f0, op1=f1), [reg(a), reg(b)], [reg(o)])
+
+    def act(o, a, fn, scale=1.0, bias=0.0, acc=None):
+        rd, wr = [], [reg(o)]
+        x, s, b = src(a, rd), src(scale, rd), src(bias, rd)
+        if acc is None:
+            op("S", lambda: g.scalar.activation(out=v(o), in_=x, func=fn, bias=b, scale=s), rd, wr)
+        else:
+            op("S", lambda: g.scalar.activation(out=v(o), in_=x, func=fn, bias=b, scale=s, accum_out=v(acc)), rd, wr + [reg(acc)])
+
+    def mms(o, *pairs):
+        n = len(pairs)
+        for j, (l, r) in enumerate(pairs):
+            r = reg(r)
+            rap = T[r[0]][:, r[1] + r[3]:r[2]:r[4]] if len(r) == 5 else v(r)
+            op("P", lambda: g.tensor.matmul(out=v(o), lhsT=v(l), rhs=rap, start=j == 0, stop=j == n - 1), [reg(l), r[:3]], [reg(o)])
+
+    def iota(o, pattern, base, cm, small=False):
+        if small:
+            op("G", lambda: g.iota(v(o), pattern, base, cm, allow_small_or_imprecise_dtypes=True), [], [reg(o)])
+        else:
+            op("G", lambda: g.iota(v(o), pattern, base, cm), [], [reg(o)])
+
+    def rowsum(b, r, i, base=0):
+        return ((b, base + 15 - i, base + 143 - i), r + (i, 16))
+
+    def POOL(t, lo, hi):
+        return ("POOL", t * POOLW + lo, t * POOLW + hi)
+
+    AND, SHR, ADD, SUB, MUL, MIN, MAX = Op.bitwise_and, Op.logical_shift_right, Op.add, Op.subtract, Op.mult, Op.min, Op.max
+    EQ, NE, GE, GT, LT, LE = Op.is_equal, Op.not_equal, Op.is_ge, Op.is_gt, Op.is_lt, Op.is_le
+
+    mate, far = T.cores[rank ^ 1], T.cores[rank ^ 4]
+    fe = topo.engines(core, far)
+    me = [e for e in topo.engines(core, mate) if e not in fe][:len(fe)]
+    half = len(fe) // 2
+
+    def transfer(dst, es, sem, a, b):
+        rid, pid = topo.addr(dst, core)
+        return RemoteDMATransfer(dst_ids=[DstId(rid=rid, pnc=pid)], dma_engine_mask=sum(1 << e for e in es), remote_sem=T.sem[sem], src=v(a), dst=v(b))
+    sent = len(fe) + len(me)
+
+    for q, sem, b, x in (("Y", "dG", "GL", T.gd[:, :]), ("S", "dW", "wi", T.wt[:, :]), ("Y", "dX", "X:0:2048", T.xs[:, 0:2048]),
+                         ("S", "dX2", "X:2048:4096", T.xs[:, 2048:4096]), ("S", "dK", "ki", T.km[:, :]), ("S", "dT", "ti", T.th[:, :]),
+                         ("Y", "dR", "R0", T.xs[0:128:16, :])):
+        dma(q, sem, v(b), x, [], [reg(b)])
+
+    iota("IP", [[0, 1]], 0, 1)
+    iota("IZ", [[1, 144]], -15, 0)
+    iota("IQ", [[1, 144]], 0, 0)
+    iota("IJ", [[16, 80]], 0, 0)
+    iota("R48", [[1, 48]], 2049, 0, True)
+    iota("RI", [[1, 48]], 0, 0, True)
+    iota("I256", [[1, 256]], 0, 0)
+    iota("IO", [[1, 256]], 0, 0, True)
+    IQ = "IQ:0:128"
+    ts("IPa", "IP", 15, AND)
+    ts("IPb", "IP", 4, SHR)
+    cp("Pf", "IP")
+    cp("PG", "IPb")
+    cp("PI", "IPa")
+    ts("P16", "PG", 16.0, MUL)
+    ts("IQa", IQ, 4, SHR)
+    ts("Z1", "IZ", "P16", EQ)
+    ts("B", "IQa", "PG", EQ)
+    cp("wf", "wi")
+    cp("wb", "wi")
+    mms("P3:0:3", ("B", "wb"))
+    for t in range(RO):
+        ts(R("ZW", 144 * t, 144 * t + 144), "Z1", R("wf", t, t + 1), MUL)
+    ts(POOL(0, 192, 192 + S), "GL", -255.0, ADD)
+    ts("SW", "P3:0:3", 255.0, MUL)
+    cp("KF", "ki")
+    ts("TH", "ti", 64.0, MUL)
+
+    LORD = [int(x[1:]) for x in SCHED if x[0] == "L"]
+
+    def prod(m):
+        b, o = ((6, 0), (7, 0), (1, 0), (1, 192))[LORD.index(m // 3)]
+        return R("P%d" % b, o + 64 * (m % 3), o + 64 * (m % 3) + 64)
+
+    def ulist(t):
+        mms("P2:0:64", *[rowsum("ZW", POOL(t, 192, 192 + S), i, 144 * t) for i in range(16)])
+        ts("u0", "P2:0:64", R("SW", t, t + 1), ADD)
+        ts("UW:0:64", "u0", 4095, AND)
+        cp("uf", "UW:0:64")
+        tt("f0", "UW:0:64", "UW:0:64", MUL)
+        for m in [3 * j + q for j in LORD for q in range(3)]:
+            act(prod(m), "uf", Fn.Copy, scale=R("KF", m, m + 1))
+        ts("FW:0:64", "f0", 5, SHR)
+
+    def clist(j):
+        lo, hi = 192 * j, 192 * j + 192
+        for q in range(3):
+            tt(R("CI", lo + 64 * q, lo + 64 * q + 64), prod(3 * j + q), "FW:0:64", ADD)
+        ts(R("CM", lo, hi), R("CI", lo, hi), 4095, AND)
+        cp(R("CL", lo, hi), R("CM", lo, hi))
+        ts(R("BI", lo, hi), R("CL", lo, hi), 4000.0, GE)
+
+    def consts1():
+        ts("ID", IQ, "Pf", EQ)
+        ts("Z64", "Z1", 64.0, MUL)
+        ts("Z128", "Z1", 128.0, MUL)
+        ts("ZN", "Z1", -64.0, MUL)
+        for m in range(M):
+            fill(R("C2", 64 * m, 64 * m + 64), 2.0 * m)
+
+    def consts2():
+        cp("BF", "B")
+        ts("NB", "B", -1.0, MUL)
+        ts("NI", "ID", -1.0, MUL)
+        ts("tA", IQ, "Pf", GT, -1.0, MUL)
+        ts("tC", IQ, "Pf", LT, -1.0, MUL)
+        ts("IQb", IQ, 15, AND)
+        ts("WI", "IQ:0:96", 15, AND)
+        ts("tB", "ID", 1024.0, MUL)
+        tt("TN", "tA", "B", MUL)
+        tt("tC", "tC", "B", MUL)
+        ts("tA", "IQa", 16.0, MUL)
+        tt("TS", "tB", "TN", ADD)
+        ts("tB", "ID", 2048.0, MUL)
+        ts("B0", "tA", "Pf", EQ, 4.0, MUL)
+        tt("TQ", "tB", "tC", ADD)
+        ts("tB", "TN", 2.0, MUL)
+        ts("tA", "IQb", 1000.0, ADD)
+        tt("TG", "tB", "NI", ADD)
+        ts("WM", "WI", "PI", EQ)
+        tt("tC", "tA", "B", MUL)
+        ts("SLW", "IJ", "PI", ADD)
+        ts("AG", "tC", -1000.0, ADD)
+        ts("P256", "PI", 256.0, MUL)
+        ts("RBH", "SLW:0:3", 0.5, ADD)
+        ts("RC", "SLW:0:3", -1.0, MUL, 832.0, ADD)
+        ts("PL", "I256", "P256", ADD)
+        ts("BM", "I256:0:16", "PI", LE, 16384.0, MUL)
+        ts("EG:0", "PI", 3.0, GE, 5000.0, MUL)
+        ts("EG:1", "PI", 0.0, EQ, -1.0, MUL)
+        ts("EG:2", "PI", 1.0, GE, -1.0, MUL)
+        tt("junk:0:12", "WM:0:12", "KF", MUL)
+        fill("ZER", 0.0)
+        tr("KD", "junk:0:12", ADD)
+        for b in ("UW", "FW", "KW"):
+            fill(R(b, 64, 80), 0)
+        fill("Q:64:80", 0.0)
+        fill("CB", 0.0)
+        for t in range(RO):
+            fill(R("SND", 384 * t, 384 * t + 384), 0.0)
+            fill(POOL(t, 192 + S, POOLW), 0.0)
+
+    def utable():
+        ts("NK", "R0", 192.0, LT)
+        scan("TU", "NK", "PL", 32768.0, MUL, MAX, True)
+        ts("fw", "WM:0:16", "TU:0", MUL)
+        mms("P7:0:16", ("BF", "fw"))
+        tt("junk:16:32", "P7:0:16", "BM", ADD)
+        tr("nf", "junk:16:32", MIN)
+        ts("UT", "TU", "nf", MIN, 4095.0, MIN)
+
+    def three(f, o, w, a):
+        o, a = reg(o), reg(a)
+        for k in range(3):
+            f(sub(o, k, k + 1), sub(a, w * k, w * k + w))
+
+    def vsum(o, a):
+        tr(o, a, ADD)
+
+    def ssum(o, a):
+        act(R("junk", 64 * (o[1] % 3), 64 * (o[1] % 3) + 16), a, Fn.Copy, acc=o)
+
+    for t in range(RO):
+        own = POOL(t, 192, 192 + S)
+        ulist(t)
+        if t == 0:
+            consts1()
+        order = [x for x in SCHED if x[:2] == "PK"]
+        for it in SCHED:
+            kind = it.rstrip("0123456789")
+            m = int(it[len(kind):])
+            Zm, Am, Cl = R("Z", S * m, S * m + S), R("A", S * m, S * m + S), R("CL", 64 * m, 64 * m + 64)
+            if kind == "L":
+                clist(m)
+            elif kind == "VG":
+                tt(Zm, ("X", Cl), own, ADD)
+            elif kind == "VR":
+                ts(Am, Zm, 0.0, MAX)
+            elif kind == "SG":
+                act(Zm, ("X", Cl), Fn.Copy)
+            elif kind == "SV":
+                act(Am, Zm, Fn.Abs)
+            elif kind in ("PX", "SA"):
+                for h in range(2):
+                    o, lo = "P%d" % (2 + h + 2 * (SMS.index(m) % 2)), 512 * h
+                    if kind == "PX":
+                        mms(o, ("ID", sub(own, lo, lo + 512)), ("ID", sub(Zm, lo, lo + 512)))
+                    else:
+                        act(sub(Am, lo, lo + 512), o, Fn.Abs)
+            elif kind == "PK":
+                n = order.index(it)
+                pairs = [("ID", R(b, 64 * m, 64 * m + 64)) for b in ("C2", "BI")]
+                for b, x in (("ZN", Zm), ("Z128", Am)) if m in RMS else (("Z64", Am),):
+                    pairs += [rowsum(b, x, i) for i in range(16)]
+                mms(R("P%d" % (n // 6), 64 * (n % 6), 64 * (n % 6) + 64), *pairs)
+            elif m == 0:
+                cp("cur", "P0:0:192")
+                tt("cur", "cur", "P0:192:384", MIN)
+                if t == 0:
+                    consts2()
+                    utable()
+            else:
+                tt("cur", "cur", "P1:0:192", MIN)
+                tt("cur", "cur", "P1:192:384", MIN)
+        tt("fa", "cur:0:64", "cur:64:128", MIN)
+        tt("KW:0:64", "fa", "cur:128:192", MIN)
+        ts("fb", "KW:0:64", 1, AND)
+        ts("fa", "KW:0:64", "TH", LT)
+        tt("FB", "fa", "fb", GT)
+        mms("P2:0:64", ("B", "FB"))
+        mms("P3:0:64", ("TQ", "FB"))
+        scan("Cs", "P2:0:64", "ZER", 0.0, ADD, ADD)
+        for k in range(3):
+            act(R("junk", 64 * k, 64 * k + 64), "Cs", Fn.Sign, scale=-1.0, bias=R("RBH", k, k + 1), acc=R("sA", k, k + 1))
+        tt("Q:0:64", "Cs", "P3:0:64", ADD)
+        ts("RV", "RI", "Cs:63", GE, 1048576.0, MUL)
+        ts("vl", "SLW:0:3", "Cs:63", LT)
+        tt("RV", "RV", "RI", ADD)
+        so = "sO:0:3"
+        ts(so, "sA", 0.5, MUL, 32.0, ADD)
+        tt("OH", ("Q", so), "R48", EQ)
+        tt("M1:0:48", ("KW", so), "OH", MUL)
+        mms("P4:0:48", ("BF", "M1:0:48"))
+        for j, b in enumerate(("UW", "FW", "SLW")):
+            tt(R("M1", 48 * j + 48, 48 * j + 96), (b, so), "OH", MUL)
+        mms("P5:0:144", ("BF", "M1:48:192"))
+        act("US", "P5:0:144", Fn.Copy)
+        cp("kI", "P4:0:48")
+        ts("mI", "kI", 1, SHR, 15, AND)
+        ts("dm", "kI", 0x7FFFC0, AND)
+        ts("xk", "mI", "PI", EQ, "KD", MUL)
+        mms("P6:0:48", ("BF", "xk"))
+        tt("CK:48:96", "dm", "RV", ADD)
+        tt("tk", "P6:0:48", "US:0:48", MUL)
+        tt("ts", "tk", "US:48:96", ADD)
+        ts("CK:0:48", "ts", 4095, AND)
+        tt("CKm", "CK", "WM", MUL)
+        three(ssum, "kw", 16, "CKm:48:96")
+        three(vsum, "cw", 16, "CKm:0:48")
+        ts("p1", "CK:0:48", 16.0, ADD)
+        ts("q1", "cw", 16.0, ADD)
+        ts("p1h", "p1", 8, SHR)
+        ts("q1l", "q1", 255, AND)
+        ts("sel", "p1h", "PI", EQ)
+        cp("qO:0:3", "q1l")
+        tt("T1", ("UT", "qO:0:3"), "sel", MUL)
+        mms("P7:0:48", ("BF", "T1"))
+        for k in range(3):
+            ts(R("tm", 48 * k, 48 * k + 48), "CK:0:48", R("cw", k, k + 1), NE, 2097152.0, MUL)
+        for k in range(3):
+            tt(R("tm", 48 * k, 48 * k + 48), R("tm", 48 * k, 48 * k + 48), "CK:48:96", ADD)
+        tt("em", "P7:0:48", "WM:0:48", MUL)
+        ts("p1", "P7:0:48", 8.0, ADD, 4095.0, MIN)
+        three(vsum, "ew:0:3", 16, "em")
+        ts("p1h", "p1", 8, SHR)
+        ts("q1", "ew:0:3", 8.0, ADD, 4095.0, MIN)
+        ts("sel", "p1h", "PI", EQ)
+        ts("q1l", "q1", 255, AND)
+        cp("qO:0:3", "q1l")
+        tt("T1", ("UT", "qO:0:3"), "sel", MUL)
+        mms("P7:0:48", ("BF", "T1"))
+        three(lambda o, a: tr(o, a, MIN), "mn", 48, "tm")
+        tt("eq", "mn", "kw", EQ)
+        tt("CB:2:5", "eq", "vl", MUL)
+        mms("P3:0:1", ("B", "CB:2"), ("B", "CB:3"), ("B", "CB:4"))
+        mms("P2:0:3", ("TS", "CB:2:5"), ("NB", "CB:1:4"), ("NB", "CB:0:3"))
+        ts("OFF:0:3", "cw", 10.0, ADD)
+        cp("OFF:3:6", "ew:0:3")
+        tt("em", "P7:0:48", "WM:0:48", MUL)
+        three(vsum, "ew:3:6", 16, "em")
+        cn = R("CN", t, t + 1)
+        cp(cn, "P3:0:1")
+        cp("OFF:6:9", "ew:3:6")
+        waits("G", [cn], [])
+        g.remote_dma_fused([transfer(far, fe, "cn%d" % t, cn, R("CNL", 2 * t + 1, 2 * t + 2)),
+                            transfer(mate, me, "cn%d" % t, cn, R("CNL", 2 * t, 2 * t + 1))], local_sem=T.sem.lsem)
+        arrive("cn%d" % t, sent, [R("CNL", 2 * t, 2 * t + 2)])
+        cp("GX", ("X", "OFF:0:9"))
+        ts("GN", "GX", 0.0, MIN)
+        mms("P5:0:144", ("NI", "GX"), ("B0", "GN"))
+        tt("vv", "P2:0:3", "RC", MAX)
+        for b in range(3):
+            ts(R("DL", 3 * b, 3 * b + 3), "vv", -1.0, MUL, 1024.0 + 64 * b, ADD)
+        tt("SLm", "US:96:144", "WM:0:48", MUL)
+        ts("GV", "P5:0:144", -255.0, MAX)
+        snd = R("SND", 384 * t, 384 * t + 384)
+        scatter(snd, "DL:0:9", "GV")
+        waits("G", [snd], [])
+        g.remote_dma_fused([transfer(far, fe[:half], "ar%d" % t, sub(snd, 64, 128), POOL(t, 64, 128)),
+                            transfer(far, fe[half:], "ar%d" % t, sub(snd, 128, 192), POOL(t, 128, 192)),
+                            transfer(mate, me, "ar%d" % t, sub(snd, 0, 64), POOL(t, 0, 64))], local_sem=T.sem.lsem)
+        arrive("ar%d" % t, sent, [POOL(t, 0, 192)])
+        three(ssum, "sw", 16, "SLm")
+        ts("nc", "CB:2:5", -100.0, MUL, 100.0, ADD)
+        cp("CE:0:3", "cw")
+        ts("CE:3:6", "ew:3:6", 1.0, ADD)
+        ts("CE:12:18", "CE:0:6", 255, AND)
+        ts("CE:6:12", "CE:0:6", 8, SHR)
+        ts("CF:6:9", "CE:12:15", -1.0, MUL, 0.5, ADD)
+        ts("CF:9:12", "CE:15:18", 0.5, SUB)
+        tt("CF:0:3", "CE:6:9", "nc", ADD)
+        tt("CF:3:6", "CE:9:12", "nc", ADD)
+        LHk = [R("LH", 128 * k, 128 * k + 128) for k in range(6)]
+        RHk = [R("RH", 256 * k, 256 * k + 256) for k in range(6)]
+        for k in range(6):
+            act(RHk[k], "IO", Fn.Sign, scale=1.0 if k < 3 else -1.0, bias=R("CF", 6 + k, 7 + k))
+            ts(LHk[k], "AG", R("CF", k, k + 1), EQ)
+        mms("P7:0:256", *zip(LHk, RHk))
+        cp("sl16:0:3", "sw")
+        cp("tg", (own, "sl16:0:3"))
+        scatter(POOL(t, 192 + S, POOLW), "DL:0:3", "tg")
+        ts("n5", "CB:2:5", -5000.0, MUL, 5000.0, ADD)
+        tt("pv", "sw", "vv", ADD)
+        tt("pv", "pv", "n5", ADD)
+        cp("lc", "P7:255")
+        mms("P3:0:1", ("TG", "lc"))
+        ts("P7:0:256", "P7:0:256", "P3:0:1", GT, -32768.0 / 2 ** t, MUL)
+        tt("R0", "R0", "P7:0:256", ADD)
+        if t < RO - 1:
+            dma("Y", "dM%d" % t, T.X[0:128:16, :], T.R0[:], [R("R0")], [R("X")])
+        n1, n2 = R("CNL", 2 * t, 2 * t + 1), R("CNL", 2 * t + 1, 2 * t + 2)
+        ts("ac:0", n2, 2.0, MUL, n1, ADD)
+        ts("PO:3", n2, "PI", MUL, "EG:0", ADD)
+        ts("ac:1", n1, "EG:1", MUL, 64.0, ADD)
+        ts("PO:0:3", "pv", "ac:0", ADD, -1024.0, ADD)
+        ts("PO:3", "PO:3", n1, ADD)
+        ts("wt4", n2, "EG:2", MUL, "ac:1", ADD)
+        cp("PJ:0:4", "PO")
+        ts("PJ:4:8", "PJ:0:4", 15, AND)
+        ts("PJ:8:12", "PJ:0:4", 4, SHR)
+        cp("PF:4:12", "PJ:4:12")
+        pairs = []
+        for k in range(4):
+            a, b, hi = sub(RHk[k], 0, 64), sub(RHk[k], 64, 128), R("PF", 8 + k, 9 + k)
+            w = ("wt4", MUL) if k == 3 else ()
+            ts(LHk[k], "AG", R("PF", 4 + k, 5 + k), GE)
+            ts(a, "IO:0:64", hi, EQ, *w)
+            ts(b, "IO:0:64", hi, GT, *w)
+            pairs += [(LHk[k], a), ("B", b)]
+        mms("P6:0:64", *pairs)
+        tt("lf", "P6:0:64", "SLW:0:64", ADD)
+        cp("LST", "lf")
+        pool = POOL(t, 0, POOLW)
+        if t < RO - 1:
+            utable()
+            nxt = POOL(t + 1, 192, 192 + S)
+            cp(sub(nxt, 0, 512), (pool, "LST:0:32"))
+            act(sub(nxt, 512, 1024), (pool, "LST:32:64"), Fn.Copy)
+        else:
+            a, b, c = "yct:0:256", "yct:256:512", "yct:512:768"
+            ts(a, "R0", -7000.0, LT, 3.0, MUL)
+            ts(b, "R0", -16000.0, LT)
+            ts(c, "R0", -32000.0, LT)
+            tt(a, a, b, SUB)
+            tt(c, a, c, SUB)
+            dma("Y", "dC", T.yc[:, :], v(c), [reg(c)], [])
+            ts("YG:0:512", (pool, "LST:0:32"), 255.0, ADD)
+            act("YG:512:1024", (pool, "LST:32:64"), Fn.Copy, bias=255.0)
+            dma("Y", "dY0", T.yg[:, 0:512], T.YG[:, 0:512], [R("YG", 0, 512)], [])
+            dma("S", "dY1", T.yg[:, 512:1024], T.YG[:, 512:1024], [R("YG", 512, 1024)], [])
+    g.wait_ge(T.sem.lsem, 2 * RO * sent)
+    for e, n in list(cnt.items()) + [(d, 16) for d in LOADS]:
+        g.wait_ge(T.sem["s" + e if e in cnt else e], n)

@@ -31,10 +31,8 @@ for _b in range(8):
 LOADS = ["dG", "dW", "dK", "dT", "dX", "dX2", "dR", "dM0", "dM1", "dY0", "dY1", "dC"]
 SEMAPHORES = ["sV", "sS", "sP", "sG", "lsem", "cn0", "cn1", "cn2", "ar0", "ar1", "ar2"] + LOADS
 
-SMS = (3, 9, 0, 6)
-RMS = (8, 10, 11)
-SCHED = """L1 SG3 L3 L2 VG11 L0 SG9 PX3 PX9 SA3 VR11 VG7 VG2 PK11 VG8 SG0 SA9 SG6 PX0 PK3 PK9 SA0 PX6 SV7 VG5 PK0 VR8 SV2 PK7 VG10 SV5
- SA6 PK8 VG4 PK2 VR10 PK5 PK10 SV4 PK6 PK4 VG1 SV1 N0 PK1 N1""".split()
+SMS = (0, 1, 3, 6)
+RMS = (10, 11)
 
 
 def R(b, lo=0, hi=None):
@@ -53,15 +51,78 @@ def sub(r, lo, hi):
     return (r[0], r[1] + lo, r[1] + hi)
 
 
+WAKE, CYC, GATHER, SLACK = 0.12, 1.04e-3, 1.5, 0.10
+HINT = ("70690956734305710000481046038848816640467591711230022104017675328880136010280030539001099740670010066529098900272740130964245400960150"
+        "00000020006610644101037627811634110158961060483100842302800369975007465029067060473050080002661004960900012225525030007030210")
+TWO = {_k for _t in (_BF, _U16) for _k in _t.split()}
+ORDERS = {}
+
+
+def psum(b):
+    return b[0] == "P" and b[1:] in "01234567" and len(b) == 2
+
+
+def plan(nodes):
+    n, hist = len(nodes), {}
+    pre, suc = [set() for _ in nodes], [[] for _ in nodes]
+    for i, x in enumerate(nodes):
+        for regs, wr in ((x["rd"], False), (x["wr"], True)):
+            for b, lo, hi in regs:
+                for l, h, w, j, q in hist.get(b, ()):
+                    if (l < hi and lo < h and (w or wr)) or (psum(b) and q != x["q"]):
+                        pre[i].add(j)
+        if x["dep"] is not None:
+            pre[i].add(x["dep"])
+        pre[i].discard(i)
+        for regs, wr in ((x["rd"], False), (x["wr"], True)):
+            for b, lo, hi in regs:
+                h = hist.setdefault(b, [])
+                if wr and not psum(b):
+                    h[:] = [e for e in h if not (lo <= e[0] and e[1] <= hi)]
+                h.append((lo, hi, wr, i, x["q"]))
+        for j in pre[i]:
+            suc[j].append(i)
+    prio = [0.0] * n
+    for i in range(n - 1, -1, -1):
+        prio[i] = nodes[i]["dur"] + nodes[i]["lat"] + max([prio[j] + WAKE for j in suc[i]], default=0.0)
+    prio = [p + 0.5 * int(HINT[x["key"]]) if 0 <= x["key"] < len(HINT) else p for p, x in zip(prio, nodes)]
+    left, rdy = [len(p) for p in pre], [0.0] * n
+    ready, free, order = {}, {}, []
+    for i in range(n):
+        if not left[i]:
+            ready.setdefault(nodes[i]["q"], []).append(i)
+    while len(order) < n:
+        best = None
+        for q, l in ready.items():
+            if not l:
+                continue
+            f = free.get(q, 0.0)
+            t = min(max(f, rdy[i]) for i in l) + SLACK
+            i = max((i for i in l if max(f, rdy[i]) <= t), key=lambda i: (prio[i], -i))
+            s = max(f, rdy[i])
+            if best is None or s < best[0]:
+                best = (s, q, i)
+        s, q, i = best
+        ready[q].remove(i)
+        order.append(i)
+        if q != "R":
+            free[q] = s + nodes[i]["dur"]
+        end = s + nodes[i]["dur"] + nodes[i]["lat"] + WAKE
+        for j in suc[i]:
+            rdy[j] = max(rdy[j], end)
+            left[j] -= 1
+            if not left[j]:
+                ready.setdefault(nodes[j]["q"], []).append(j)
+    return order
+
+
 def builder(g, T):
     eng = {"V": g.vector, "S": g.scalar, "P": g.tensor, "G": g, "Y": g.sync}
     cnt = {"V": 0, "S": 0, "P": 0, "G": 0}
     know = {q: {} for q in eng}
     snap = {}
     hist = {}
-
-    def psum(b):
-        return b[0] == "P" and b[1:] in "01234567" and len(b) == 2
+    nodes, key = [], [0]
 
     def wait(q, reads, writes):
         want = {}
@@ -91,31 +152,62 @@ def builder(g, T):
                                              ((x[3] == e and x[2] == wr) or (wr and not psum(b))))]
                 h.append([lo, hi, wr, e, c])
 
-    def op(q, call, reads, writes):
-        wait(q, reads, writes)
-        call().then_inc(T.sem["s" + q], 1)
-        cnt[q] += 1
-        snap[(q, cnt[q])] = dict(know[q])
-        log(reads, writes, q, cnt[q])
+    def add(q, calls, rd, wr, dur, lat=0.0, sem=None, val=16, dep=None):
+        nodes.append({"q": q, "calls": calls, "rd": rd, "wr": wr, "dur": dur, "lat": lat, "sem": sem, "val": val, "dep": dep, "key": key[0]})
+        key[0] += 1
+        return len(nodes) - 1
 
-    def dma(q, sem, out, in_, reads, writes):
-        wait(q, reads, writes)
-        eng[q].dma_start(out=out, in_=in_).then_inc(T.sem[sem], 16)
-        snap[(sem, 16)] = dict(know[q])
-        log(reads, writes, sem, 16)
+    def emit():
+        if "order" not in ORDERS:
+            ORDERS["order"] = plan(nodes)
+        for i in ORDERS["order"]:
+            x = nodes[i]
+            q, sem = x["q"], x["sem"]
+            if q == "R":
+                log([], x["wr"], sem, x["val"])
+                continue
+            wait(q, x["rd"], x["wr"])
+            for j, call in enumerate(x["calls"]):
+                ins = call()
+                if sem is None and j == len(x["calls"]) - 1:
+                    ins.then_inc(T.sem["s" + q], 1)
+                    cnt[q] += 1
+                    snap[(q, cnt[q])] = dict(know[q])
+                    log(x["rd"], x["wr"], q, cnt[q])
+                elif sem is not None and sem[0] == "d":
+                    ins.then_inc(T.sem[sem], 16)
+                    snap[(sem, 16)] = dict(know[q])
+                    log(x["rd"], x["wr"], sem, 16)
 
-    def arrive(sem, val, writes):
-        log([], writes, sem, val)
+    def count(k):
+        old, key[0] = key[0], k
+        return old
 
-    return op, dma, arrive, wait, cnt
+    return add, emit, cnt, count
 
 
 def rank_program(g, core, T, topo):
     rank = T.rank_of(core)
     if rank is None:
         return
-    op, dma, arrive, waits, cnt = builder(g, T)
+    add, emit, cnt, count = builder(g, T)
     V = g.vector
+
+    def op(q, call, rd, wr, cycles, plus=0.0):
+        add(q, [call], rd, wr, plus + max(64, cycles) * CYC)
+
+    def dma(q, sem, out, in_, rd, wr, us=3.5):
+        add(q, [lambda: (g.sync if q == "Y" else g.scalar).dma_start(out=out, in_=in_)], rd, wr, 0.1, us, sem)
+
+    def size(r):
+        r = reg(r)
+        return r[2] - r[1]
+
+    def inds(*xs):
+        return any(isinstance(x, tuple) and len(x) == 2 for x in xs)
+
+    def small(*xs):
+        return all(reg(x)[0] in TWO for x in xs)
 
     def v(r):
         r = reg(r)
@@ -139,54 +231,58 @@ def rank_program(g, core, T, topo):
     def tt(o, a, b, f):
         rd = []
         x, y = src(a, rd), src(b, rd)
-        op("V", lambda: V.tensor_tensor(out=v(o), in0=x, in1=y, op=f), rd, [reg(o)])
+        op("V", lambda: V.tensor_tensor(out=v(o), in0=x, in1=y, op=f), rd, [reg(o)],
+           size(o) * (GATHER if inds(a, b) else 1 if any(psum(r[0]) for r in rd + [reg(o)]) else 2), 0.06 * inds(a, b))
 
     def ts(o, a, s1, f0, s2=None, f1=None):
         rd = []
         x, y, z = src(a, rd), src(s1, rd), src(s2, rd)
+        c = size(o) * (GATHER if inds(a) else 0.5 if small(o, a) else 1)
         if f1 is None:
-            op("V", lambda: V.tensor_scalar(out=v(o), in0=x, scalar1=y, scalar2=None, op0=f0), rd, [reg(o)])
+            op("V", lambda: V.tensor_scalar(out=v(o), in0=x, scalar1=y, scalar2=None, op0=f0), rd, [reg(o)], c)
         else:
-            op("V", lambda: V.tensor_scalar(out=v(o), in0=x, scalar1=y, scalar2=z, op0=f0, op1=f1), rd, [reg(o)])
+            op("V", lambda: V.tensor_scalar(out=v(o), in0=x, scalar1=y, scalar2=z, op0=f0, op1=f1), rd, [reg(o)], c)
 
     def cp(o, a):
         rd = []
         x = src(a, rd)
-        op("V", lambda: V.tensor_copy(out=v(o), in_=x), rd, [reg(o)])
+        op("V", lambda: V.tensor_copy(out=v(o), in_=x), rd, [reg(o)], size(o) * (GATHER if inds(a) else 0.5 if small(o, a) else 1))
 
     def scatter(win, lst, a):
-        op("V", lambda: V.tensor_copy(out=v(win).indirect(v(lst)), in_=v(a)), [reg(a), reg(lst)], [win])
+        op("V", lambda: V.tensor_copy(out=v(win).indirect(v(lst)), in_=v(a)), [reg(a), reg(lst)], [win], 3.8 * size(a))
 
     def tr(o, a, f):
-        op("V", lambda: V.tensor_reduce(out=v(o), in_=v(a), axis=AxisListType.X, op=f), [reg(a)], [reg(o)])
+        op("V", lambda: V.tensor_reduce(out=v(o), in_=v(a), axis=AxisListType.X, op=f), [reg(a)], [reg(o)], size(a))
 
     def fill(o, x):
-        op("V", lambda: V.memset(v(o), x), [], [reg(o)])
+        op("V", lambda: V.memset(v(o), x), [], [reg(o)], size(o))
 
     def scan(o, a, b, ini, f0, f1, turn=False):
         w = back if turn else v
-        op("V", lambda: V.tensor_tensor_scan(out=w(o), data0=w(a), data1=w(b), initial=ini, op0=f0, op1=f1), [reg(a), reg(b)], [reg(o)])
+        op("V", lambda: V.tensor_tensor_scan(out=w(o), data0=w(a), data1=w(b), initial=ini, op0=f0, op1=f1), [reg(a), reg(b)], [reg(o)], size(o))
 
     def act(o, a, fn, scale=1.0, bias=0.0, acc=None):
         rd, wr = [], [reg(o)]
         x, s, b = src(a, rd), src(scale, rd), src(bias, rd)
         if acc is None:
-            op("S", lambda: g.scalar.activation(out=v(o), in_=x, func=fn, bias=b, scale=s), rd, wr)
+            op("S", lambda: g.scalar.activation(out=v(o), in_=x, func=fn, bias=b, scale=s), rd, wr, size(o) * (GATHER if inds(a) else 1), 0.03)
         else:
-            op("S", lambda: g.scalar.activation(out=v(o), in_=x, func=fn, bias=b, scale=s, accum_out=v(acc)), rd, wr + [reg(acc)])
+            op("S", lambda: g.scalar.activation(out=v(o), in_=x, func=fn, bias=b, scale=s, accum_out=v(acc)), rd, wr + [reg(acc)], size(o), 0.05)
 
     def mms(o, *pairs):
-        n = len(pairs)
-        for j, (l, r) in enumerate(pairs):
-            r = reg(r)
+        def one(j, l, r):
             rap = T[r[0]][:, r[1] + r[3]:r[2]:r[4]] if len(r) == 5 else v(r)
-            op("P", lambda: g.tensor.matmul(out=v(o), lhsT=v(l), rhs=rap, start=j == 0, stop=j == n - 1), [reg(l), r[:3]], [reg(o)])
+            return lambda: g.tensor.matmul(out=v(o), lhsT=v(l), rhs=rap, start=j == 0, stop=j == len(pairs) - 1)
+        pairs = [(reg(l), reg(r)) for l, r in pairs]
+        four = 1 if pairs[0][1][0] in TWO else 4
+        add("P", [one(j, l, r) for j, (l, r) in enumerate(pairs)], [p for l, r in pairs for p in (l, r[:3])], [reg(o)],
+            max(64, size(o)) * four * len(pairs) * 0.5e-3)
 
     def iota(o, pattern, base, cm, small=False):
         if small:
-            op("G", lambda: g.iota(v(o), pattern, base, cm, allow_small_or_imprecise_dtypes=True), [], [reg(o)])
+            op("G", lambda: g.iota(v(o), pattern, base, cm, allow_small_or_imprecise_dtypes=True), [], [reg(o)], 2 * size(o), 0.13)
         else:
-            op("G", lambda: g.iota(v(o), pattern, base, cm), [], [reg(o)])
+            op("G", lambda: g.iota(v(o), pattern, base, cm), [], [reg(o)], 2 * size(o), 0.13)
 
     def rowsum(b, r, i, base=0):
         return ((b, base + 15 - i, base + 143 - i), r + (i, 16))
@@ -207,6 +303,11 @@ def rank_program(g, core, T, topo):
         return RemoteDMATransfer(dst_ids=[DstId(rid=rid, pnc=pid)], dma_engine_mask=sum(1 << e for e in es), remote_sem=T.sem[sem], src=v(a), dst=v(b))
     sent = len(fe) + len(me)
 
+    def send(sem, transfers, a, land):
+        i = add("G", [lambda: g.remote_dma_fused(transfers, local_sem=T.sem.lsem)], [a], [], 1.0, sem="rem")
+        add("R", [], [], [land], 0.0, 2.2, sem, sent, i)
+
+    count(-1000)
     for q, sem, b, x in (("Y", "dG", "GL", T.gd[:, :]), ("S", "dW", "wi", T.wt[:, :]), ("Y", "dX", "X:0:2048", T.xs[:, 0:2048]),
                          ("S", "dX2", "X:2048:4096", T.xs[:, 2048:4096]), ("S", "dK", "ki", T.km[:, :]), ("S", "dT", "ti", T.th[:, :]),
                          ("Y", "dR", "R0", T.xs[0:128:16, :])):
@@ -240,10 +341,8 @@ def rank_program(g, core, T, topo):
     cp("KF", "ki")
     ts("TH", "ti", 64.0, MUL)
 
-    LORD = [int(x[1:]) for x in SCHED if x[0] == "L"]
-
     def prod(m):
-        b, o = ((6, 0), (7, 0), (1, 0), (1, 192))[LORD.index(m // 3)]
+        b, o = ((6, 0), (7, 0), (1, 0), (1, 192))[m // 3]
         return R("P%d" % b, o + 64 * (m % 3), o + 64 * (m % 3) + 64)
 
     def ulist(t):
@@ -252,7 +351,7 @@ def rank_program(g, core, T, topo):
         ts("UW:0:64", "u0", 4095, AND)
         cp("uf", "UW:0:64")
         tt("f0", "UW:0:64", "UW:0:64", MUL)
-        for m in [3 * j + q for j in LORD for q in range(3)]:
+        for m in range(M):
             act(prod(m), "uf", Fn.Copy, scale=R("KF", m, m + 1))
         ts("FW:0:64", "f0", 5, SHR)
 
@@ -336,46 +435,41 @@ def rank_program(g, core, T, topo):
 
     for t in range(RO):
         own = POOL(t, 192, 192 + S)
+        count(0)
         ulist(t)
         if t == 0:
+            k = count(-1000)
             consts1()
-        order = [x for x in SCHED if x[:2] == "PK"]
-        for it in SCHED:
-            kind = it.rstrip("0123456789")
-            m = int(it[len(kind):])
+            count(k)
+        for j in range(4):
+            clist(j)
+        for m in range(M):
             Zm, Am, Cl = R("Z", S * m, S * m + S), R("A", S * m, S * m + S), R("CL", 64 * m, 64 * m + 64)
-            if kind == "L":
-                clist(m)
-            elif kind == "VG":
-                tt(Zm, ("X", Cl), own, ADD)
-            elif kind == "VR":
-                ts(Am, Zm, 0.0, MAX)
-            elif kind == "SG":
+            if m in SMS:
                 act(Zm, ("X", Cl), Fn.Copy)
-            elif kind == "SV":
-                act(Am, Zm, Fn.Abs)
-            elif kind in ("PX", "SA"):
                 for h in range(2):
                     o, lo = "P%d" % (2 + h + 2 * (SMS.index(m) % 2)), 512 * h
-                    if kind == "PX":
-                        mms(o, ("ID", sub(own, lo, lo + 512)), ("ID", sub(Zm, lo, lo + 512)))
-                    else:
-                        act(sub(Am, lo, lo + 512), o, Fn.Abs)
-            elif kind == "PK":
-                n = order.index(it)
-                pairs = [("ID", R(b, 64 * m, 64 * m + 64)) for b in ("C2", "BI")]
-                for b, x in (("ZN", Zm), ("Z128", Am)) if m in RMS else (("Z64", Am),):
-                    pairs += [rowsum(b, x, i) for i in range(16)]
-                mms(R("P%d" % (n // 6), 64 * (n % 6), 64 * (n % 6) + 64), *pairs)
-            elif m == 0:
-                cp("cur", "P0:0:192")
-                tt("cur", "cur", "P0:192:384", MIN)
-                if t == 0:
-                    consts2()
-                    utable()
+                    mms(o, ("ID", sub(own, lo, lo + 512)), ("ID", sub(Zm, lo, lo + 512)))
+                    act(sub(Am, lo, lo + 512), o, Fn.Abs)
             else:
-                tt("cur", "cur", "P1:0:192", MIN)
-                tt("cur", "cur", "P1:192:384", MIN)
+                tt(Zm, ("X", Cl), own, ADD)
+                if m in RMS:
+                    ts(Am, Zm, 0.0, MAX)
+                else:
+                    act(Am, Zm, Fn.Abs)
+            pairs = [("ID", R(b, 64 * m, 64 * m + 64)) for b in ("C2", "BI")]
+            for b, x in (("ZN", Zm), ("Z128", Am)) if m in RMS else (("Z64", Am),):
+                pairs += [rowsum(b, x, i) for i in range(16)]
+            mms(R("P%d" % (m // 6), 64 * (m % 6), 64 * (m % 6) + 64), *pairs)
+        if t == 0:
+            k = count(-1000)
+            consts2()
+            utable()
+            count(k)
+        cp("cur", "P0:0:192")
+        tt("cur", "cur", "P0:192:384", MIN)
+        tt("cur", "cur", "P1:0:192", MIN)
+        tt("cur", "cur", "P1:192:384", MIN)
         tt("fa", "cur:0:64", "cur:64:128", MIN)
         tt("KW:0:64", "fa", "cur:128:192", MIN)
         ts("fb", "KW:0:64", 1, AND)
@@ -445,10 +539,8 @@ def rank_program(g, core, T, topo):
         cn = R("CN", t, t + 1)
         cp(cn, "P3:0:1")
         cp("OFF:6:9", "ew:3:6")
-        waits("G", [cn], [])
-        g.remote_dma_fused([transfer(far, fe, "cn%d" % t, cn, R("CNL", 2 * t + 1, 2 * t + 2)),
-                            transfer(mate, me, "cn%d" % t, cn, R("CNL", 2 * t, 2 * t + 1))], local_sem=T.sem.lsem)
-        arrive("cn%d" % t, sent, [R("CNL", 2 * t, 2 * t + 2)])
+        send("cn%d" % t, [transfer(far, fe, "cn%d" % t, cn, R("CNL", 2 * t + 1, 2 * t + 2)),
+                          transfer(mate, me, "cn%d" % t, cn, R("CNL", 2 * t, 2 * t + 1))], cn, R("CNL", 2 * t, 2 * t + 2))
         cp("GX", ("X", "OFF:0:9"))
         ts("GN", "GX", 0.0, MIN)
         mms("P5:0:144", ("NI", "GX"), ("B0", "GN"))
@@ -459,11 +551,9 @@ def rank_program(g, core, T, topo):
         ts("GV", "P5:0:144", -255.0, MAX)
         snd = R("SND", 384 * t, 384 * t + 384)
         scatter(snd, "DL:0:9", "GV")
-        waits("G", [snd], [])
-        g.remote_dma_fused([transfer(far, fe[:half], "ar%d" % t, sub(snd, 64, 128), POOL(t, 64, 128)),
-                            transfer(far, fe[half:], "ar%d" % t, sub(snd, 128, 192), POOL(t, 128, 192)),
-                            transfer(mate, me, "ar%d" % t, sub(snd, 0, 64), POOL(t, 0, 64))], local_sem=T.sem.lsem)
-        arrive("ar%d" % t, sent, [POOL(t, 0, 192)])
+        send("ar%d" % t, [transfer(far, fe[:half], "ar%d" % t, sub(snd, 64, 128), POOL(t, 64, 128)),
+                          transfer(far, fe[half:], "ar%d" % t, sub(snd, 128, 192), POOL(t, 128, 192)),
+                          transfer(mate, me, "ar%d" % t, sub(snd, 0, 64), POOL(t, 0, 64))], snd, POOL(t, 0, 192))
         three(ssum, "sw", 16, "SLm")
         ts("nc", "CB:2:5", -100.0, MUL, 100.0, ADD)
         cp("CE:0:3", "cw")
@@ -532,6 +622,7 @@ def rank_program(g, core, T, topo):
             act("YG:512:1024", (pool, "LST:32:64"), Fn.Copy, bias=255.0)
             dma("Y", "dY0", T.yg[:, 0:512], T.YG[:, 0:512], [R("YG", 0, 512)], [])
             dma("S", "dY1", T.yg[:, 512:1024], T.YG[:, 512:1024], [R("YG", 512, 1024)], [])
+    emit()
     g.wait_ge(T.sem.lsem, 2 * RO * sent)
     for e, n in list(cnt.items()) + [(d, 16) for d in LOADS]:
         g.wait_ge(T.sem["s" + e if e in cnt else e], n)

@@ -3,14 +3,15 @@ from concourse.mybir import AluOpType as Op, AxisListType, ActivationFunctionTyp
 
 RO, M, S, W, CAP = 3, 12, 1024, 4096, 48
 POOLW = 192 + S + 240
-_F32 = """wf 3 KF 12 TH 1 KD 1 SW 3 Pf 1 PI 1 PG 1 P16 1 P256 1 BF 128 tA 128 tB 128 tC 128 WM 96 R48 48 RI 48 SLW 80 RBH 3 RC 3 PL 256
- BM 16 EG 4 ZER 64 uf 64 Q 80 cur 192 fa 64 Cs 64 junk 192 sA 3 OH 48 M1 192 xk 48 US 144 tk 48 RV 48 vl 3 CKm 96 SLm 48 cw 3 kw 3 sw 3
- tm 144 mn 3 eq 3 vv 3 nc 3 n5 3 pv 3 sel 48 T1 48 em 48 ew 6 UT 256 TU 256 fw 16 nf 1 wt4 1 CF 12 PO 4 ac 2 PF 12 lf 64
- yct 768 CN 3 CNL 6"""
+_F32 = """wf 3 KF 12 TH 1 KD 1 SW 3 Pf 1 PI 1 PG 1 P16 1 P256 1 BF 128 tA 128 tB 128 tC 128 tD 128 tE 128 WM 96 R48 48 RI 48 SLW 80 RBH 3 RC 3
+ PL 256 BM 16 EG 4 ZER 64 uf 64 Q 80 cur 192 fa 64 Cs 64 junk 192 sA 3 OH 48 M1 192 xk 48 US 144 tk 48 RV 48 vl 3 CKm 96 SLm 48 cw 3 kw 3 sw 3
+ tm 144 mn 3 eq 3 vv 3 nc 3 n5 3 pv 3 sel 48 T1 48 em 48 ew 6 UT 256 TU 256 fw 16 nf 1 wt4 1 CF 12 PO 4 ac 3 PF 4 lf 64
+ yct 256 YB 3 CN 3 CNL 6"""
 _BF = """X 4096 GL 1024 YG 1024 Z 12288 A 12288 wb 3 Z1 144 Z64 144 Z128 144 ZN 144 ZW 432 B 128 NB 128 ID 128 NI 128 TN 128 TS 128 TQ 128
- B0 128 TG 128 AG 128 IO 256 BI 768 C2 768 FB 64 CB 8 GX 144 GN 144 GV 144 LH 768 RH 1536 lc 1 R0 256 NK 256 tg 48 SND 1152 POOL 4368"""
+ B0 128 TG 128 Y3 128 Y1 128 AG 128 AGp 128 IO16 64 IO 256 BI 768 C2 768 FB 64 CB 8 GX 144 GN 144 GV 144 LH 1024 RH 1536 lc 1 R0 256 NK 256
+ tg 48 SND 1152 POOL 4368"""
 _I32 = """wi 3 ki 12 ti 1 IP 1 IPa 1 IPb 1 IQ 144 IQa 128 IQb 128 IZ 144 IJ 80 I256 256 WI 96 UW 80 FW 80 KW 80 u0 64 f0 64 CI 768 CM 768
- fb 64 kI 48 mI 48 dm 48 ts 48 CK 96 p1 48 p1h 48 q1 3 q1l 3 CE 18 PJ 12"""
+ fb 64 kI 48 mI 48 dm 48 ts 48 CK 96 p1 48 p1h 48 q1 3 q1l 3 CE 18 PJ 8"""
 _U16 = "CL 768 sO 4 DL 12 OFF 12 qO 4 LST 64 sl16 4"
 COLS, SCRATCH, PLACE = {}, {}, {}
 for _txt, _dt in ((_F32, "float32"), (_BF, "bfloat16"), (_I32, "int32"), (_U16, "uint16")):
@@ -32,7 +33,7 @@ LOADS = ["dG", "dW", "dK", "dT", "dX", "dX2", "dR", "dM0", "dM1", "dY0", "dY1", 
 SEMAPHORES = ["sV", "sS", "sP", "sG", "lsem", "cn0", "cn1", "cn2", "ar0", "ar1", "ar2"] + LOADS
 
 SMS = (0, 1, 3, 6)
-RMS = (10, 11)
+RMS = (9, 10, 11)
 
 
 def R(b, lo=0, hi=None):
@@ -52,8 +53,8 @@ def sub(r, lo, hi):
 
 
 WAKE, CYC, GATHER, SLACK = 0.12, 1.04e-3, 1.5, 0.10
-HINT = ("70690956734305710000481046038848816640467591711230022104017675328880136010280030539001099740670010066529098900272740130964245400960150"
-        "00000020006610644101037627811634110158961060483100842302800369975007465029067060473050080002661004960900012225525030007030210")
+HINT = ("04063769656271386045144780815589920545733890020253425010900001080800440909354774405107808900080800275990981087050920792303210856000859"
+        "020324062016193719011460005540009729252008968738078207900107450755950678724219169209800513049000919002101803720839245550202005003002061")
 TWO = {_k for _t in (_BF, _U16) for _k in _t.split()}
 ORDERS = {}
 
@@ -71,8 +72,7 @@ def plan(nodes):
                 for l, h, w, j, q in hist.get(b, ()):
                     if (l < hi and lo < h and (w or wr)) or (psum(b) and q != x["q"]):
                         pre[i].add(j)
-        if x["dep"] is not None:
-            pre[i].add(x["dep"])
+        pre[i].update(x["dep"])
         pre[i].discard(i)
         for regs, wr in ((x["rd"], False), (x["wr"], True)):
             for b, lo, hi in regs:
@@ -152,8 +152,8 @@ def builder(g, T):
                                              ((x[3] == e and x[2] == wr) or (wr and not psum(b))))]
                 h.append([lo, hi, wr, e, c])
 
-    def add(q, calls, rd, wr, dur, lat=0.0, sem=None, val=16, dep=None):
-        nodes.append({"q": q, "calls": calls, "rd": rd, "wr": wr, "dur": dur, "lat": lat, "sem": sem, "val": val, "dep": dep, "key": key[0]})
+    def add(q, calls, rd, wr, dur, lat=0.0, sem=None, val=16, dep=()):
+        nodes.append({"q": q, "calls": calls, "rd": rd, "wr": wr, "dur": dur, "lat": lat, "sem": sem, "val": val, "dep": tuple(dep), "key": key[0]})
         key[0] += 1
         return len(nodes) - 1
 
@@ -254,9 +254,6 @@ def rank_program(g, core, T, topo):
     def tr(o, a, f):
         op("V", lambda: V.tensor_reduce(out=v(o), in_=v(a), axis=AxisListType.X, op=f), [reg(a)], [reg(o)], size(a))
 
-    def fill(o, x):
-        op("V", lambda: V.memset(v(o), x), [], [reg(o)], size(o))
-
     def scan(o, a, b, ini, f0, f1, turn=False):
         w = back if turn else v
         op("V", lambda: V.tensor_tensor_scan(out=w(o), data0=w(a), data1=w(b), initial=ini, op0=f0, op1=f1), [reg(a), reg(b)], [reg(o)], size(o))
@@ -269,20 +266,23 @@ def rank_program(g, core, T, topo):
         else:
             op("S", lambda: g.scalar.activation(out=v(o), in_=x, func=fn, bias=b, scale=s, accum_out=v(acc)), rd, wr + [reg(acc)], size(o), 0.05)
 
-    def mms(o, *pairs):
+    def mms(o, *pairs, start=True, stop=True, dep=()):
         def one(j, l, r):
             rap = T[r[0]][:, r[1] + r[3]:r[2]:r[4]] if len(r) == 5 else v(r)
-            return lambda: g.tensor.matmul(out=v(o), lhsT=v(l), rhs=rap, start=j == 0, stop=j == len(pairs) - 1)
+            return lambda: g.tensor.matmul(out=v(o), lhsT=v(l), rhs=rap, start=start and j == 0, stop=stop and j == len(pairs) - 1)
         pairs = [(reg(l), reg(r)) for l, r in pairs]
         four = 1 if pairs[0][1][0] in TWO else 4
-        add("P", [one(j, l, r) for j, (l, r) in enumerate(pairs)], [p for l, r in pairs for p in (l, r[:3])], [reg(o)],
-            max(64, size(o)) * four * len(pairs) * 0.5e-3)
+        return add("P", [one(j, l, r) for j, (l, r) in enumerate(pairs)], [p for l, r in pairs for p in (l, r[:3])], [reg(o)],
+                   max(64, size(o)) * four * len(pairs) * 0.5e-3, dep=dep)
 
     def iota(o, pattern, base, cm, small=False):
         if small:
             op("G", lambda: g.iota(v(o), pattern, base, cm, allow_small_or_imprecise_dtypes=True), [], [reg(o)], 2 * size(o), 0.13)
         else:
             op("G", lambda: g.iota(v(o), pattern, base, cm), [], [reg(o)], 2 * size(o), 0.13)
+
+    def zero(o):
+        iota(o, [[0, size(o)]], 0, 0, reg(o)[0] not in ("UW", "FW", "KW"))
 
     def rowsum(b, r, i, base=0):
         return ((b, base + 15 - i, base + 143 - i), r + (i, 16))
@@ -305,7 +305,7 @@ def rank_program(g, core, T, topo):
 
     def send(sem, transfers, a, land):
         i = add("G", [lambda: g.remote_dma_fused(transfers, local_sem=T.sem.lsem)], [a], [], 1.0, sem="rem")
-        add("R", [], [], [land], 0.0, 2.2, sem, sent, i)
+        add("R", [], [], [land], 0.0, 2.2, sem, sent, (i,))
 
     count(-1000)
     for q, sem, b, x in (("Y", "dG", "GL", T.gd[:, :]), ("S", "dW", "wi", T.wt[:, :]), ("Y", "dX", "X:0:2048", T.xs[:, 0:2048]),
@@ -321,6 +321,14 @@ def rank_program(g, core, T, topo):
     iota("RI", [[1, 48]], 0, 0, True)
     iota("I256", [[1, 256]], 0, 0)
     iota("IO", [[1, 256]], 0, 0, True)
+    iota("C2", [[2, 12], [0, 64]], 0, 0, True)
+    for b in ("UW:64:80", "FW:64:80", "KW:64:80", "Q:64:80", "ZER", "CB"):
+        zero(b)
+    for k in range(3):
+        iota(R("YB", k, k + 1), [[0, 1]], (-7000, -16000, -32000)[k], 0, True)
+    for t in range(RO):
+        zero(R("SND", 384 * t, 384 * t + 192))
+        zero(POOL(t, 192 + S, POOLW))
     IQ = "IQ:0:128"
     ts("IPa", "IP", 15, AND)
     ts("IPb", "IP", 4, SHR)
@@ -365,35 +373,39 @@ def rank_program(g, core, T, topo):
 
     def consts1():
         ts("ID", IQ, "Pf", EQ)
-        ts("Z64", "Z1", 64.0, MUL)
-        ts("Z128", "Z1", 128.0, MUL)
-        ts("ZN", "Z1", -64.0, MUL)
-        for m in range(M):
-            fill(R("C2", 64 * m, 64 * m + 64), 2.0 * m)
+        act("Z64", "Z1", Fn.Copy, scale=64.0)
+        act("Z128", "Z1", Fn.Copy, scale=128.0)
+        act("ZN", "Z1", Fn.Copy, scale=-64.0)
 
     def consts2():
-        cp("BF", "B")
-        ts("NB", "B", -1.0, MUL)
-        ts("NI", "ID", -1.0, MUL)
+        act("BF", "B", Fn.Copy)
+        act("NB", "B", Fn.Copy, scale=-1.0)
+        act("NI", "ID", Fn.Copy, scale=-1.0)
+        act("Y3", "ID", Fn.Copy, scale=1.5)
+        act("Y1", "ID", Fn.Copy, scale=-0.5)
         ts("tA", IQ, "Pf", GT, -1.0, MUL)
         ts("tC", IQ, "Pf", LT, -1.0, MUL)
         ts("IQb", IQ, 15, AND)
         ts("WI", "IQ:0:96", 15, AND)
-        ts("tB", "ID", 1024.0, MUL)
+        act("tB", "ID", Fn.Copy, scale=1024.0)
         tt("TN", "tA", "B", MUL)
         tt("tC", "tC", "B", MUL)
         ts("tA", "IQa", 16.0, MUL)
         tt("TS", "tB", "TN", ADD)
-        ts("tB", "ID", 2048.0, MUL)
+        act("tD", "ID", Fn.Copy, scale=2048.0)
         ts("B0", "tA", "Pf", EQ, 4.0, MUL)
-        tt("TQ", "tB", "tC", ADD)
-        ts("tB", "TN", 2.0, MUL)
+        tt("TQ", "tD", "tC", ADD)
+        act("tE", "TN", Fn.Copy, scale=2.0)
         ts("tA", "IQb", 1000.0, ADD)
-        tt("TG", "tB", "NI", ADD)
+        tt("TG", "tE", "NI", ADD)
         ts("WM", "WI", "PI", EQ)
         tt("tC", "tA", "B", MUL)
         ts("SLW", "IJ", "PI", ADD)
         ts("AG", "tC", -1000.0, ADD)
+        ts("tA", "IQb", -1000.0, ADD)
+        act("IO16", "IO:0:64", Fn.Copy, scale=16.0)
+        tt("tA", "tA", "B", MUL)
+        ts("AGp", "tA", 1000.0, ADD)
         ts("P256", "PI", 256.0, MUL)
         ts("RBH", "SLW:0:3", 0.5, ADD)
         ts("RC", "SLW:0:3", -1.0, MUL, 832.0, ADD)
@@ -403,15 +415,7 @@ def rank_program(g, core, T, topo):
         ts("EG:1", "PI", 0.0, EQ, -1.0, MUL)
         ts("EG:2", "PI", 1.0, GE, -1.0, MUL)
         tt("junk:0:12", "WM:0:12", "KF", MUL)
-        fill("ZER", 0.0)
         tr("KD", "junk:0:12", ADD)
-        for b in ("UW", "FW", "KW"):
-            fill(R(b, 64, 80), 0)
-        fill("Q:64:80", 0.0)
-        fill("CB", 0.0)
-        for t in range(RO):
-            fill(R("SND", 384 * t, 384 * t + 384), 0.0)
-            fill(POOL(t, 192 + S, POOLW), 0.0)
 
     def utable():
         ts("NK", "R0", 192.0, LT)
@@ -443,6 +447,9 @@ def rank_program(g, core, T, topo):
             count(k)
         for j in range(4):
             clist(j)
+        parts = {}
+        for b, m, n in ((0, 0, 6), (1, 6, 3), (6, 9, 3)):
+            parts[b] = [mms(R("P%d" % b, 0, 64 * n), *[("ID", R(x, 64 * m, 64 * (m + n))) for x in ("C2", "BI")], stop=False)]
         for m in range(M):
             Zm, Am, Cl = R("Z", S * m, S * m + S), R("A", S * m, S * m + S), R("CL", 64 * m, 64 * m + 64)
             if m in SMS:
@@ -457,10 +464,11 @@ def rank_program(g, core, T, topo):
                     ts(Am, Zm, 0.0, MAX)
                 else:
                     act(Am, Zm, Fn.Abs)
-            pairs = [("ID", R(b, 64 * m, 64 * m + 64)) for b in ("C2", "BI")]
-            for b, x in (("ZN", Zm), ("Z128", Am)) if m in RMS else (("Z64", Am),):
-                pairs += [rowsum(b, x, i) for i in range(16)]
-            mms(R("P%d" % (m // 6), 64 * (m % 6), 64 * (m % 6) + 64), *pairs)
+            b, n, last = (0, m, m == 5) if m < 6 else (1, m - 6, m == 8) if m < 9 else (6, m - 9, m == 11)
+            for z, x in (("ZN", Zm), ("Z128", Am)) if m in RMS else (("Z64", Am),):
+                stop = last and x is Am
+                parts[b].append(mms(R("P%d" % b, 64 * n, 64 * n + 64), *[rowsum(z, x, i) for i in range(16)],
+                                    start=False, stop=stop, dep=parts[b] if stop else ()))
         if t == 0:
             k = count(-1000)
             consts2()
@@ -469,7 +477,7 @@ def rank_program(g, core, T, topo):
         cp("cur", "P0:0:192")
         tt("cur", "cur", "P0:192:384", MIN)
         tt("cur", "cur", "P1:0:192", MIN)
-        tt("cur", "cur", "P1:192:384", MIN)
+        tt("cur", "cur", "P6:0:192", MIN)
         tt("fa", "cur:0:64", "cur:64:128", MIN)
         tt("KW:0:64", "fa", "cur:128:192", MIN)
         ts("fb", "KW:0:64", 1, AND)
@@ -564,7 +572,7 @@ def rank_program(g, core, T, topo):
         ts("CF:9:12", "CE:15:18", 0.5, SUB)
         tt("CF:0:3", "CE:6:9", "nc", ADD)
         tt("CF:3:6", "CE:9:12", "nc", ADD)
-        LHk = [R("LH", 128 * k, 128 * k + 128) for k in range(6)]
+        LHk = [R("LH", 128 * k, 128 * k + 128) for k in range(8)]
         RHk = [R("RH", 256 * k, 256 * k + 256) for k in range(6)]
         for k in range(6):
             act(RHk[k], "IO", Fn.Sign, scale=1.0 if k < 3 else -1.0, bias=R("CF", 6 + k, 7 + k))
@@ -584,23 +592,24 @@ def rank_program(g, core, T, topo):
             dma("Y", "dM%d" % t, T.X[0:128:16, :], T.R0[:], [R("R0")], [R("X")])
         n1, n2 = R("CNL", 2 * t, 2 * t + 1), R("CNL", 2 * t + 1, 2 * t + 2)
         ts("ac:0", n2, 2.0, MUL, n1, ADD)
-        ts("PO:3", n2, "PI", MUL, "EG:0", ADD)
+        ts("ac:2", n2, "PI", MUL, "EG:0", ADD)
         ts("ac:1", n1, "EG:1", MUL, 64.0, ADD)
         ts("PO:0:3", "pv", "ac:0", ADD, -1024.0, ADD)
-        ts("PO:3", "PO:3", n1, ADD)
+        ts("PJ:0:3", "pv", "ac:0", ADD, -1024.0, ADD)
+        ts("PJ:3", "ac:2", n1, ADD)
+        ts("PO:3", "ac:2", n1, ADD)
         ts("wt4", n2, "EG:2", MUL, "ac:1", ADD)
-        cp("PJ:0:4", "PO")
         ts("PJ:4:8", "PJ:0:4", 15, AND)
-        ts("PJ:8:12", "PJ:0:4", 4, SHR)
-        cp("PF:4:12", "PJ:4:12")
+        cp("PF", "PJ:4:8")
         pairs = []
         for k in range(4):
-            a, b, hi = sub(RHk[k], 0, 64), sub(RHk[k], 64, 128), R("PF", 8 + k, 9 + k)
+            a, b, pos, lo = sub(RHk[k], 0, 64), sub(RHk[k], 64, 128), R("PO", k, k + 1), R("PF", k, k + 1)
             w = ("wt4", MUL) if k == 3 else ()
-            ts(LHk[k], "AG", R("PF", 4 + k, 5 + k), GE)
-            ts(a, "IO:0:64", hi, EQ, *w)
-            ts(b, "IO:0:64", hi, GT, *w)
-            pairs += [(LHk[k], a), ("B", b)]
+            ts(a, "IO16", 15.0, ADD, pos, GE)
+            ts(b, "IO16", pos, GT)
+            ts(LHk[k], "AG", lo, GE, *w)
+            ts(LHk[4 + k], "AGp", lo, LT, *w)
+            pairs += [(LHk[k], a), (LHk[4 + k], b)]
         mms("P6:0:64", *pairs)
         tt("lf", "P6:0:64", "SLW:0:64", ADD)
         cp("LST", "lf")
@@ -611,13 +620,11 @@ def rank_program(g, core, T, topo):
             cp(sub(nxt, 0, 512), (pool, "LST:0:32"))
             act(sub(nxt, 512, 1024), (pool, "LST:32:64"), Fn.Copy)
         else:
-            a, b, c = "yct:0:256", "yct:256:512", "yct:512:768"
-            ts(a, "R0", -7000.0, LT, 3.0, MUL)
-            ts(b, "R0", -16000.0, LT)
-            ts(c, "R0", -32000.0, LT)
-            tt(a, a, b, SUB)
-            tt(c, a, c, SUB)
-            dma("Y", "dC", T.yc[:, :], v(c), [reg(c)], [])
+            for k in range(3):
+                act(RHk[k], "R0", Fn.Sign, scale=-1.0, bias=R("YB", k, k + 1))
+            mms("P5:0:256", ("Y3", RHk[0]), ("Y1", RHk[1]), ("Y1", RHk[2]))
+            act("yct", "P5:0:256", Fn.Copy, bias=0.5)
+            dma("Y", "dC", T.yc[:, :], v("yct"), [R("yct")], [])
             ts("YG:0:512", (pool, "LST:0:32"), 255.0, ADD)
             act("YG:512:1024", (pool, "LST:32:64"), Fn.Copy, bias=255.0)
             dma("Y", "dY0", T.yg[:, 0:512], T.YG[:, 0:512], [R("YG", 0, 512)], [])

from concourse.bass import DstId, RemoteDMATransfer
from concourse.mybir import AluOpType as Op, AxisListType, ActivationFunctionType as Fn

RO, M, S, W, CAP = 3, 12, 1024, 4096, 48
POOLW = 192 + S + 240
_F32 = """wf 3 KF 12 TH 1 KD 1 SW 3 Pf 1 PI 1 PG 1 P16 1 P256 1 BF 128 tA 128 tB 128 tC 128 tD 128 tE 128 WM 96 R48 48 RI 48 SLW 80 RBH 3 RC 3
 PL 256 BM 16 EG 4 ZER 64 uf 64 Q 80 cur 192 fa 64 Cs 64 junk 192 sA 3 OH 48 M1 192 xk 48 US 144 tk 48 RV 48 vl 3 CKm 96 SLm 48 cw 3 kw 3 sw 3
 tm 144 mn 3 eq 3 vv 3 nc 3 n5 3 pv 3 sel 48 T1 48 em 48 ew 6 UT 256 TU 256 fw 16 nf 1 wt4 1 CF 12 PO 4 ac 3 PF 4 lf 64
 yct 256 YB 3 CN 3 CNL 6"""
_BF = """X 4096 GL 1024 YG 1024 Z 12288 A 12288 wb 3 Z1 144 Z64 144 Z128 144 ZN 144 ZW 432 B 128 NB 128 ID 128 NI 128 TN 128 TS 128 TQ 128
 B0 128 TG 128 Y3 128 Y1 128 AG 128 AGp 128 IO16 64 IO 256 BI 768 C2 768 FB 64 CB 8 GX 144 GN 144 GV 144 LH 1024 RH 1536 lc 1 R0 256 NK 256
 tg 48 SND 1152 POOL 4368"""
_I32 = """wi 3 ki 12 ti 1 IP 1 IPa 1 IPb 1 IQ 144 IQa 128 IQb 128 IZ 144 IJ 80 I256 256 WI 96 UW 80 FW 80 KW 80 u0 64 f0 64 CI 768 CM 768
 fb 64 kI 48 mI 48 dm 48 ts 48 CK 96 p1 48 p1h 48 q1 3 q1l 3 CE 18 PJ 8"""
_U16 = "CL 768 sO 4 DL 12 OFF 12 qO 4 LST 64 sl16 4"
COLS, SCRATCH, PLACE = {}, {}, {}
for _txt, _dt in ((_F32, "float32"), (_BF, "bfloat16"), (_I32, "int32"), (_U16, "uint16")):
    _w, _at = _txt.split(), 16
    for _k in range(0, len(_w), 2):
        _n = int(_w[_k + 1])
        COLS[_w[_k]] = _n
        if _dt == "bfloat16" or _w[_k] in ("CN", "CNL"):
            SCRATCH[_w[_k]] = ("sbuf", [128, _n], _dt)
        else:
            PLACE[_w[_k]] = ("all_" + _dt, _at)
            _at += _n + (-_n) % 16
    if _dt != "bfloat16":
        SCRATCH["all_" + _dt] = ("sbuf", [128, _at], _dt)
for _b in range(8):
    SCRATCH["P%d" % _b] = ("psum", [128, 512], "float32")
    COLS["P%d" % _b] = 512
LOADS = ["dG", "dW", "dK", "dT", "dX", "dX2", "dR", "dM0", "dM1", "dY0", "dY1", "dC"]
SEMAPHORES = ["sV", "sS", "sP", "sG", "lsem", "cn0", "cn1", "cn2", "ar0", "ar1", "ar2"] + LOADS

SMS = (0, 1, 3, 6)
RMS = (9, 10, 11)


def R(b, lo=0, hi=None):
    return (b, lo, COLS[b] if hi is None else hi)


def reg(x):
    if not isinstance(x, str):
        return x
    p = x.split(":")
    lo = int(p[1]) if len(p) > 1 else 0
    return (p[0], lo, int(p[2]) if len(p) > 2 else lo + 1 if len(p) > 1 else COLS[p[0]])


def sub(r, lo, hi):
    return (r[0], r[1] + lo, r[1] + hi)


WAKE, CYC, GATHER, SLACK = 0.12, 1.04e-3, 1.5, 0.10
HINT = ("04063769656271386045144780815589920545733890020253425010900001080800440909354774405107808900080800275990981087050920792303210856000859"
        "020324062016193719011460005540009729252008968738078207900107450755950678724219169209800513049000919002101803720839245550202005003002061")
TWO = {_k for _t in (_BF, _U16) for _k in _t.split()}
ORDERS = {}


def psum(b):
    return b[0] == "P" and b[1:] in "01234567" and len(b) == 2


def plan(nodes):
    n, hist = len(nodes), {}
    pre, suc = [set() for _ in nodes], [[] for _ in nodes]
    for i, x in enumerate(nodes):
        for regs, wr in ((x["rd"], False), (x["wr"], True)):
            for b, lo, hi in regs:
                for l, h, w, j, q in hist.get(b, ()):
                    if (l < hi and lo < h and (w or wr)) or (psum(b) and q != x["q"]):
                        pre[i].add(j)
        pre[i].update(x["dep"])
        pre[i].discard(i)
        for regs, wr in ((x["rd"], False), (x["wr"], True)):
            for b, lo, hi in regs:
                h = hist.setdefault(b, [])
                if wr and not psum(b):
                    h[:] = [e for e in h if not (lo <= e[0] and e[1] <= hi)]
                h.append((lo, hi, wr, i, x["q"]))
        for j in pre[i]:
            suc[j].append(i)
    prio = [0.0] * n
    for i in range(n - 1, -1, -1):
        prio[i] = nodes[i]["dur"] + nodes[i]["lat"] + max([prio[j] + WAKE for j in suc[i]], default=0.0)
    prio = [p + 0.5 * int(HINT[x["key"]]) if 0 <= x["key"] < len(HINT) else p for p, x in zip(prio, nodes)]
    left, rdy = [len(p) for p in pre], [0.0] * n
    ready, free, order = {}, {}, []
    for i in range(n):
        if not left[i]:
            ready.setdefault(nodes[i]["q"], []).append(i)
    while len(order) < n:
        best = None
        for q, l in ready.items():
            if not l:
                continue
            f = free.get(q, 0.0)
            t = min(max(f, rdy[i]) for i in l) + SLACK
            i = max((i for i in l if max(f, rdy[i]) <= t), key=lambda i: (prio[i], -i))
            s = max(f, rdy[i])
            if best is None or s < best[0]:
                best = (s, q, i)
        s, q, i = best
        ready[q].remove(i)
        order.append(i)
        if q != "R":
            free[q] = s + nodes[i]["dur"]
        end = s + nodes[i]["dur"] + nodes[i]["lat"] + WAKE
        for j in suc[i]:
            rdy[j] = max(rdy[j], end)
            left[j] -= 1
            if not left[j]:
                ready.setdefault(nodes[j]["q"], []).append(j)
    return order


def builder(g, T):
    eng = {"V": g.vector, "S": g.scalar, "P": g.tensor, "G": g, "Y": g.sync}
    cnt = {"V": 0, "S": 0, "P": 0, "G": 0}
    know = {q: {} for q in eng}
    snap = {}
    hist = {}
    nodes, key = [], [0]

    def wait(q, reads, writes):
        want = {}
        for regs, wr in ((reads, False), (writes, True)):
            for b, lo, hi in regs:
                ps = psum(b)
                for h in hist.get(b, ()):
                    same = h[3] == q
                    if same and q == "P":
                        continue
                    over = h[0] < hi and lo < h[1]
                    if ((ps and not same) or (over and (h[2] or wr))) and want.get(h[3], 0) < h[4]:
                        want[h[3]] = h[4]
        for e, c in sorted(want.items(), key=lambda x: (x[0] == q, x[0])):
            k = know[q]
            if k.get(e, 0) < c:
                eng[q].wait_ge(T.sem["s" + e if e in cnt else e], c)
                for e2, c2 in list(snap.get((e, c), {}).items()) + [(e, c)]:
                    if k.get(e2, 0) < c2:
                        k[e2] = c2

    def log(reads, writes, e, c):
        for regs, wr in ((reads, False), (writes, True)):
            for b, lo, hi in regs:
                h = hist.setdefault(b, [])
                h[:] = [x for x in h if not (lo <= x[0] and x[1] <= hi and
                                             ((x[3] == e and x[2] == wr) or (wr and not psum(b))))]
                h.append([lo, hi, wr, e, c])

    def add(q, calls, rd, wr, dur, lat=0.0, sem=None, val=16, dep=()):
        nodes.append({"q": q, "calls": calls, "rd": rd, "wr": wr, "dur": dur, "lat": lat, "sem": sem, "val": val, "dep": tuple(dep), "key": key[0]})
        key[0] += 1
        return len(nodes) - 1

    def emit():
        if "order" not in ORDERS:
            ORDERS["order"] = plan(nodes)
        for i in ORDERS["order"]:
            x = nodes[i]
            q, sem = x["q"], x["sem"]
            if q == "R":
                log([], x["wr"], sem, x["val"])
                continue
            wait(q, x["rd"], x["wr"])
            for j, call in enumerate(x["calls"]):
                ins = call()
                if sem is None and j == len(x["calls"]) - 1:
                    ins.then_inc(T.sem["s" + q], 1)
                    cnt[q] += 1
                    snap[(q, cnt[q])] = dict(know[q])
                    log(x["rd"], x["wr"], q, cnt[q])
                elif sem is not None and sem[0] == "d":
                    ins.then_inc(T.sem[sem], 16)
                    snap[(sem, 16)] = dict(know[q])
                    log(x["rd"], x["wr"], sem, 16)

    def count(k):
        old, key[0] = key[0], k
        return old

    return add, emit, cnt, count


def rank_program(g, core, T, topo):
    rank = T.rank_of(core)
    if rank is None:
        return
    add, emit, cnt, count = builder(g, T)
    V = g.vector

    def op(q, call, rd, wr, cycles, plus=0.0):
        add(q, [call], rd, wr, plus + max(64, cycles) * CYC)

    def dma(q, sem, out, in_, rd, wr, us=3.5):
        add(q, [lambda: (g.sync if q == "Y" else g.scalar).dma_start(out=out, in_=in_)], rd, wr, 0.1, us, sem)

    def size(r):
        r = reg(r)
        return r[2] - r[1]

    def inds(*xs):
        return any(isinstance(x, tuple) and len(x) == 2 for x in xs)

    def small(*xs):
        return all(reg(x)[0] in TWO for x in xs)

    def v(r):
        r = reg(r)
        b, o = PLACE.get(r[0], (r[0], 0))
        return T[b][:, o + r[1]:o + r[2]]

    def back(b):
        n, (b, o) = COLS[b], PLACE.get(b, (b, 0))
        return T[b][:, o + n - 1:(o - 1 if o else None):-1]

    def src(x, rd):
        if isinstance(x, tuple) and len(x) == 2:
            a, b = reg(x[0]), reg(x[1])
            rd += [a, b]
            return v(a).indirect(v(b))
        if isinstance(x, (tuple, str)):
            rd.append(reg(x))
            return v(x)
        return x

    def tt(o, a, b, f):
        rd = []
        x, y = src(a, rd), src(b, rd)
        op("V", lambda: V.tensor_tensor(out=v(o), in0=x, in1=y, op=f), rd, [reg(o)],
           size(o) * (GATHER if inds(a, b) else 1 if any(psum(r[0]) for r in rd + [reg(o)]) else 2), 0.06 * inds(a, b))

    def ts(o, a, s1, f0, s2=None, f1=None):
        rd = []
        x, y, z = src(a, rd), src(s1, rd), src(s2, rd)
        c = size(o) * (GATHER if inds(a) else 0.5 if small(o, a) else 1)
        if f1 is None:
            op("V", lambda: V.tensor_scalar(out=v(o), in0=x, scalar1=y, scalar2=None, op0=f0), rd, [reg(o)], c)
        else:
            op("V", lambda: V.tensor_scalar(out=v(o), in0=x, scalar1=y, scalar2=z, op0=f0, op1=f1), rd, [reg(o)], c)

    def cp(o, a):
        rd = []
        x = src(a, rd)
        op("V", lambda: V.tensor_copy(out=v(o), in_=x), rd, [reg(o)], size(o) * (GATHER if inds(a) else 0.5 if small(o, a) else 1))

    def scatter(win, lst, a):
        op("V", lambda: V.tensor_copy(out=v(win).indirect(v(lst)), in_=v(a)), [reg(a), reg(lst)], [win], 3.8 * size(a))

    def tr(o, a, f):
        op("V", lambda: V.tensor_reduce(out=v(o), in_=v(a), axis=AxisListType.X, op=f), [reg(a)], [reg(o)], size(a))

    def scan(o, a, b, ini, f0, f1, turn=False):
        w = back if turn else v
        op("V", lambda: V.tensor_tensor_scan(out=w(o), data0=w(a), data1=w(b), initial=ini, op0=f0, op1=f1), [reg(a), reg(b)], [reg(o)], size(o))

    def act(o, a, fn, scale=1.0, bias=0.0, acc=None):
        rd, wr = [], [reg(o)]
        x, s, b = src(a, rd), src(scale, rd), src(bias, rd)
        if acc is None:
            op("S", lambda: g.scalar.activation(out=v(o), in_=x, func=fn, bias=b, scale=s), rd, wr, size(o) * (GATHER if inds(a) else 1), 0.03)
        else:
            op("S", lambda: g.scalar.activation(out=v(o), in_=x, func=fn, bias=b, scale=s, accum_out=v(acc)), rd, wr + [reg(acc)], size(o), 0.05)

    def mms(o, *pairs, start=True, stop=True, dep=()):
        def one(j, l, r):
            rap = T[r[0]][:, r[1] + r[3]:r[2]:r[4]] if len(r) == 5 else v(r)
            return lambda: g.tensor.matmul(out=v(o), lhsT=v(l), rhs=rap, start=start and j == 0, stop=stop and j == len(pairs) - 1)
        pairs = [(reg(l), reg(r)) for l, r in pairs]
        four = 1 if pairs[0][1][0] in TWO else 4
        return add("P", [one(j, l, r) for j, (l, r) in enumerate(pairs)], [p for l, r in pairs for p in (l, r[:3])], [reg(o)],
                   max(64, size(o)) * four * len(pairs) * 0.5e-3, dep=dep)

    def iota(o, pattern, base, cm, small=False):
        if small:
            op("G", lambda: g.iota(v(o), pattern, base, cm, allow_small_or_imprecise_dtypes=True), [], [reg(o)], 2 * size(o), 0.13)
        else:
            op("G", lambda: g.iota(v(o), pattern, base, cm), [], [reg(o)], 2 * size(o), 0.13)

    def zero(o):
        iota(o, [[0, size(o)]], 0, 0, reg(o)[0] not in ("UW", "FW", "KW"))

    def rowsum(b, r, i, base=0):
        return ((b, base + 15 - i, base + 143 - i), r + (i, 16))

    def POOL(t, lo, hi):
        return ("POOL", t * POOLW + lo, t * POOLW + hi)

    AND, SHR, ADD, SUB, MUL, MIN, MAX = Op.bitwise_and, Op.logical_shift_right, Op.add, Op.subtract, Op.mult, Op.min, Op.max
    EQ, NE, GE, GT, LT, LE = Op.is_equal, Op.not_equal, Op.is_ge, Op.is_gt, Op.is_lt, Op.is_le

    mate, far = T.cores[rank ^ 1], T.cores[rank ^ 4]
    fe = topo.engines(core, far)
    me = [e for e in topo.engines(core, mate) if e not in fe][:len(fe)]
    half = len(fe) // 2

    def transfer(dst, es, sem, a, b):
        rid, pid = topo.addr(dst, core)
        return RemoteDMATransfer(dst_ids=[DstId(rid=rid, pnc=pid)], dma_engine_mask=sum(1 << e for e in es), remote_sem=T.sem[sem], src=v(a), dst=v(b))
    sent = len(fe) + len(me)

    def send(sem, transfers, a, land):
        i = add("G", [lambda: g.remote_dma_fused(transfers, local_sem=T.sem.lsem)], [a], [], 1.0, sem="rem")
        add("R", [], [], [land], 0.0, 2.2, sem, sent, (i,))

    count(-1000)
    for q, sem, b, x in (("Y", "dG", "GL", T.gd[:, :]), ("S", "dW", "wi", T.wt[:, :]), ("Y", "dX", "X:0:2048", T.xs[:, 0:2048]),
                         ("S", "dX2", "X:2048:4096", T.xs[:, 2048:4096]), ("S", "dK", "ki", T.km[:, :]), ("S", "dT", "ti", T.th[:, :]),
                         ("Y", "dR", "R0", T.xs[0:128:16, :])):
        dma(q, sem, v(b), x, [], [reg(b)])

    iota("IP", [[0, 1]], 0, 1)
    iota("IZ", [[1, 144]], -15, 0)
    iota("IQ", [[1, 144]], 0, 0)
    iota("IJ", [[16, 80]], 0, 0)
    iota("R48", [[1, 48]], 2049, 0, True)
    iota("RI", [[1, 48]], 0, 0, True)
    iota("I256", [[1, 256]], 0, 0)
    iota("IO", [[1, 256]], 0, 0, True)
    iota("C2", [[2, 12], [0, 64]], 0, 0, True)
    for b in ("UW:64:80", "FW:64:80", "KW:64:80", "Q:64:80", "ZER", "CB"):
        zero(b)
    for k in range(3):
        iota(R("YB", k, k + 1), [[0, 1]], (-7000, -16000, -32000)[k], 0, True)
    for t in range(RO):
        zero(R("SND", 384 * t, 384 * t + 192))
        zero(POOL(t, 192 + S, POOLW))
    IQ = "IQ:0:128"
    ts("IPa", "IP", 15, AND)
    ts("IPb", "IP", 4, SHR)
    cp("Pf", "IP")
    cp("PG", "IPb")
    cp("PI", "IPa")
    ts("P16", "PG", 16.0, MUL)
    ts("IQa", IQ, 4, SHR)
    ts("Z1", "IZ", "P16", EQ)
    ts("B", "IQa", "PG", EQ)
    cp("wf", "wi")
    cp("wb", "wi")
    mms("P3:0:3", ("B", "wb"))
    for t in range(RO):
        ts(R("ZW", 144 * t, 144 * t + 144), "Z1", R("wf", t, t + 1), MUL)
    ts(POOL(0, 192, 192 + S), "GL", -255.0, ADD)
    ts("SW", "P3:0:3", 255.0, MUL)
    cp("KF", "ki")
    ts("TH", "ti", 64.0, MUL)

    def prod(m):
        b, o = ((6, 0), (7, 0), (1, 0), (1, 192))[m // 3]
        return R("P%d" % b, o + 64 * (m % 3), o + 64 * (m % 3) + 64)

    def ulist(t):
        mms("P2:0:64", *[rowsum("ZW", POOL(t, 192, 192 + S), i, 144 * t) for i in range(16)])
        ts("u0", "P2:0:64", R("SW", t, t + 1), ADD)
        ts("UW:0:64", "u0", 4095, AND)
        cp("uf", "UW:0:64")
        tt("f0", "UW:0:64", "UW:0:64", MUL)
        for m in range(M):
            act(prod(m), "uf", Fn.Copy, scale=R("KF", m, m + 1))
        ts("FW:0:64", "f0", 5, SHR)

    def clist(j):
        lo, hi = 192 * j, 192 * j + 192
        for q in range(3):
            tt(R("CI", lo + 64 * q, lo + 64 * q + 64), prod(3 * j + q), "FW:0:64", ADD)
        ts(R("CM", lo, hi), R("CI", lo, hi), 4095, AND)
        cp(R("CL", lo, hi), R("CM", lo, hi))
        ts(R("BI", lo, hi), R("CL", lo, hi), 4000.0, GE)

    def consts1():
        ts("ID", IQ, "Pf", EQ)
        act("Z64", "Z1", Fn.Copy, scale=64.0)
        act("Z128", "Z1", Fn.Copy, scale=128.0)
        act("ZN", "Z1", Fn.Copy, scale=-64.0)

    def consts2():
        act("BF", "B", Fn.Copy)
        act("NB", "B", Fn.Copy, scale=-1.0)
        act("NI", "ID", Fn.Copy, scale=-1.0)
        act("Y3", "ID", Fn.Copy, scale=1.5)
        act("Y1", "ID", Fn.Copy, scale=-0.5)
        ts("tA", IQ, "Pf", GT, -1.0, MUL)
        ts("tC", IQ, "Pf", LT, -1.0, MUL)
        ts("IQb", IQ, 15, AND)
        ts("WI", "IQ:0:96", 15, AND)
        act("tB", "ID", Fn.Copy, scale=1024.0)
        tt("TN", "tA", "B", MUL)
        tt("tC", "tC", "B", MUL)
        ts("tA", "IQa", 16.0, MUL)
        tt("TS", "tB", "TN", ADD)
        act("tD", "ID", Fn.Copy, scale=2048.0)
        ts("B0", "tA", "Pf", EQ, 4.0, MUL)
        tt("TQ", "tD", "tC", ADD)
        act("tE", "TN", Fn.Copy, scale=2.0)
        ts("tA", "IQb", 1000.0, ADD)
        tt("TG", "tE", "NI", ADD)
        ts("WM", "WI", "PI", EQ)
        tt("tC", "tA", "B", MUL)
        ts("SLW", "IJ", "PI", ADD)
        ts("AG", "tC", -1000.0, ADD)
        ts("tA", "IQb", -1000.0, ADD)
        act("IO16", "IO:0:64", Fn.Copy, scale=16.0)
        tt("tA", "tA", "B", MUL)
        ts("AGp", "tA", 1000.0, ADD)
        ts("P256", "PI", 256.0, MUL)
        ts("RBH", "SLW:0:3", 0.5, ADD)
        ts("RC", "SLW:0:3", -1.0, MUL, 832.0, ADD)
        ts("PL", "I256", "P256", ADD)
        ts("BM", "I256:0:16", "PI", LE, 16384.0, MUL)
        ts("EG:0", "PI", 3.0, GE, 5000.0, MUL)
        ts("EG:1", "PI", 0.0, EQ, -1.0, MUL)
        ts("EG:2", "PI", 1.0, GE, -1.0, MUL)
        tt("junk:0:12", "WM:0:12", "KF", MUL)
        tr("KD", "junk:0:12", ADD)

    def utable():
        ts("NK", "R0", 192.0, LT)
        scan("TU", "NK", "PL", 32768.0, MUL, MAX, True)
        ts("fw", "WM:0:16", "TU:0", MUL)
        mms("P7:0:16", ("BF", "fw"))
        tt("junk:16:32", "P7:0:16", "BM", ADD)
        tr("nf", "junk:16:32", MIN)
        ts("UT", "TU", "nf", MIN, 4095.0, MIN)

    def three(f, o, w, a):
        o, a = reg(o), reg(a)
        for k in range(3):
            f(sub(o, k, k + 1), sub(a, w * k, w * k + w))

    def vsum(o, a):
        tr(o, a, ADD)

    def ssum(o, a):
        act(R("junk", 64 * (o[1] % 3), 64 * (o[1] % 3) + 16), a, Fn.Copy, acc=o)

    for t in range(RO):
        own = POOL(t, 192, 192 + S)
        count(0)
        ulist(t)
        if t == 0:
            k = count(-1000)
            consts1()
            count(k)
        for j in range(4):
            clist(j)
        parts = {}
        for b, m, n in ((0, 0, 6), (1, 6, 3), (6, 9, 3)):
            parts[b] = [mms(R("P%d" % b, 0, 64 * n), *[("ID", R(x, 64 * m, 64 * (m + n))) for x in ("C2", "BI")], stop=False)]
        for m in range(M):
            Zm, Am, Cl = R("Z", S * m, S * m + S), R("A", S * m, S * m + S), R("CL", 64 * m, 64 * m + 64)
            if m in SMS:
                act(Zm, ("X", Cl), Fn.Copy)
                for h in range(2):
                    o, lo = "P%d" % (2 + h + 2 * (SMS.index(m) % 2)), 512 * h
                    mms(o, ("ID", sub(own, lo, lo + 512)), ("ID", sub(Zm, lo, lo + 512)))
                    act(sub(Am, lo, lo + 512), o, Fn.Abs)
            else:
                tt(Zm, ("X", Cl), own, ADD)
                if m in RMS:
                    ts(Am, Zm, 0.0, MAX)
                else:
                    act(Am, Zm, Fn.Abs)
            b, n, last = (0, m, m == 5) if m < 6 else (1, m - 6, m == 8) if m < 9 else (6, m - 9, m == 11)
            for z, x in (("ZN", Zm), ("Z128", Am)) if m in RMS else (("Z64", Am),):
                stop = last and x is Am
                parts[b].append(mms(R("P%d" % b, 64 * n, 64 * n + 64), *[rowsum(z, x, i) for i in range(16)],
                                    start=False, stop=stop, dep=parts[b] if stop else ()))
        if t == 0:
            k = count(-1000)
            consts2()
            utable()
            count(k)
        cp("cur", "P0:0:192")
        tt("cur", "cur", "P0:192:384", MIN)
        tt("cur", "cur", "P1:0:192", MIN)
        tt("cur", "cur", "P6:0:192", MIN)
        tt("fa", "cur:0:64", "cur:64:128", MIN)
        tt("KW:0:64", "fa", "cur:128:192", MIN)
        ts("fb", "KW:0:64", 1, AND)
        ts("fa", "KW:0:64", "TH", LT)
        tt("FB", "fa", "fb", GT)
        mms("P2:0:64", ("B", "FB"))
        mms("P3:0:64", ("TQ", "FB"))
        scan("Cs", "P2:0:64", "ZER", 0.0, ADD, ADD)
        for k in range(3):
            act(R("junk", 64 * k, 64 * k + 64), "Cs", Fn.Sign, scale=-1.0, bias=R("RBH", k, k + 1), acc=R("sA", k, k + 1))
        tt("Q:0:64", "Cs", "P3:0:64", ADD)
        ts("RV", "RI", "Cs:63", GE, 1048576.0, MUL)
        ts("vl", "SLW:0:3", "Cs:63", LT)
        tt("RV", "RV", "RI", ADD)
        so = "sO:0:3"
        ts(so, "sA", 0.5, MUL, 32.0, ADD)
        tt("OH", ("Q", so), "R48", EQ)
        tt("M1:0:48", ("KW", so), "OH", MUL)
        mms("P4:0:48", ("BF", "M1:0:48"))
        for j, b in enumerate(("UW", "FW", "SLW")):
            tt(R("M1", 48 * j + 48, 48 * j + 96), (b, so), "OH", MUL)
        mms("P5:0:144", ("BF", "M1:48:192"))
        act("US", "P5:0:144", Fn.Copy)
        cp("kI", "P4:0:48")
        ts("mI", "kI", 1, SHR, 15, AND)
        ts("dm", "kI", 0x7FFFC0, AND)
        ts("xk", "mI", "PI", EQ, "KD", MUL)
        mms("P6:0:48", ("BF", "xk"))
        tt("CK:48:96", "dm", "RV", ADD)
        tt("tk", "P6:0:48", "US:0:48", MUL)
        tt("ts", "tk", "US:48:96", ADD)
        ts("CK:0:48", "ts", 4095, AND)
        tt("CKm", "CK", "WM", MUL)
        three(ssum, "kw", 16, "CKm:48:96")
        three(vsum, "cw", 16, "CKm:0:48")
        ts("p1", "CK:0:48", 16.0, ADD)
        ts("q1", "cw", 16.0, ADD)
        ts("p1h", "p1", 8, SHR)
        ts("q1l", "q1", 255, AND)
        ts("sel", "p1h", "PI", EQ)
        cp("qO:0:3", "q1l")
        tt("T1", ("UT", "qO:0:3"), "sel", MUL)
        mms("P7:0:48", ("BF", "T1"))
        for k in range(3):
            ts(R("tm", 48 * k, 48 * k + 48), "CK:0:48", R("cw", k, k + 1), NE, 2097152.0, MUL)
        for k in range(3):
            tt(R("tm", 48 * k, 48 * k + 48), R("tm", 48 * k, 48 * k + 48), "CK:48:96", ADD)
        tt("em", "P7:0:48", "WM:0:48", MUL)
        ts("p1", "P7:0:48", 8.0, ADD, 4095.0, MIN)
        three(vsum, "ew:0:3", 16, "em")
        ts("p1h", "p1", 8, SHR)
        ts("q1", "ew:0:3", 8.0, ADD, 4095.0, MIN)
        ts("sel", "p1h", "PI", EQ)
        ts("q1l", "q1", 255, AND)
        cp("qO:0:3", "q1l")
        tt("T1", ("UT", "qO:0:3"), "sel", MUL)
        mms("P7:0:48", ("BF", "T1"))
        three(lambda o, a: tr(o, a, MIN), "mn", 48, "tm")
        tt("eq", "mn", "kw", EQ)
        tt("CB:2:5", "eq", "vl", MUL)
        mms("P3:0:1", ("B", "CB:2"), ("B", "CB:3"), ("B", "CB:4"))
        mms("P2:0:3", ("TS", "CB:2:5"), ("NB", "CB:1:4"), ("NB", "CB:0:3"))
        ts("OFF:0:3", "cw", 10.0, ADD)
        cp("OFF:3:6", "ew:0:3")
        tt("em", "P7:0:48", "WM:0:48", MUL)
        three(vsum, "ew:3:6", 16, "em")
        cn = R("CN", t, t + 1)
        cp(cn, "P3:0:1")
        cp("OFF:6:9", "ew:3:6")
        send("cn%d" % t, [transfer(far, fe, "cn%d" % t, cn, R("CNL", 2 * t + 1, 2 * t + 2)),
                          transfer(mate, me, "cn%d" % t, cn, R("CNL", 2 * t, 2 * t + 1))], cn, R("CNL", 2 * t, 2 * t + 2))
        cp("GX", ("X", "OFF:0:9"))
        ts("GN", "GX", 0.0, MIN)
        mms("P5:0:144", ("NI", "GX"), ("B0", "GN"))
        tt("vv", "P2:0:3", "RC", MAX)
        for b in range(3):
            ts(R("DL", 3 * b, 3 * b + 3), "vv", -1.0, MUL, 1024.0 + 64 * b, ADD)
        tt("SLm", "US:96:144", "WM:0:48", MUL)
        ts("GV", "P5:0:144", -255.0, MAX)
        snd = R("SND", 384 * t, 384 * t + 384)
        scatter(snd, "DL:0:9", "GV")
        send("ar%d" % t, [transfer(far, fe[:half], "ar%d" % t, sub(snd, 64, 128), POOL(t, 64, 128)),
                          transfer(far, fe[half:], "ar%d" % t, sub(snd, 128, 192), POOL(t, 128, 192)),
                          transfer(mate, me, "ar%d" % t, sub(snd, 0, 64), POOL(t, 0, 64))], snd, POOL(t, 0, 192))
        three(ssum, "sw", 16, "SLm")
        ts("nc", "CB:2:5", -100.0, MUL, 100.0, ADD)
        cp("CE:0:3", "cw")
        ts("CE:3:6", "ew:3:6", 1.0, ADD)
        ts("CE:12:18", "CE:0:6", 255, AND)
        ts("CE:6:12", "CE:0:6", 8, SHR)
        ts("CF:6:9", "CE:12:15", -1.0, MUL, 0.5, ADD)
        ts("CF:9:12", "CE:15:18", 0.5, SUB)
        tt("CF:0:3", "CE:6:9", "nc", ADD)
        tt("CF:3:6", "CE:9:12", "nc", ADD)
        LHk = [R("LH", 128 * k, 128 * k + 128) for k in range(8)]
        RHk = [R("RH", 256 * k, 256 * k + 256) for k in range(6)]
        for k in range(6):
            act(RHk[k], "IO", Fn.Sign, scale=1.0 if k < 3 else -1.0, bias=R("CF", 6 + k, 7 + k))
            ts(LHk[k], "AG", R("CF", k, k + 1), EQ)
        mms("P7:0:256", *zip(LHk, RHk))
        cp("sl16:0:3", "sw")
        cp("tg", (own, "sl16:0:3"))
        scatter(POOL(t, 192 + S, POOLW), "DL:0:3", "tg")
        ts("n5", "CB:2:5", -5000.0, MUL, 5000.0, ADD)
        tt("pv", "sw", "vv", ADD)
        tt("pv", "pv", "n5", ADD)
        cp("lc", "P7:255")
        mms("P3:0:1", ("TG", "lc"))
        ts("P7:0:256", "P7:0:256", "P3:0:1", GT, -32768.0 / 2 ** t, MUL)
        tt("R0", "R0", "P7:0:256", ADD)
        if t < RO - 1:
            dma("Y", "dM%d" % t, T.X[0:128:16, :], T.R0[:], [R("R0")], [R("X")])
        n1, n2 = R("CNL", 2 * t, 2 * t + 1), R("CNL", 2 * t + 1, 2 * t + 2)
        ts("ac:0", n2, 2.0, MUL, n1, ADD)
        ts("ac:2", n2, "PI", MUL, "EG:0", ADD)
        ts("ac:1", n1, "EG:1", MUL, 64.0, ADD)
        ts("PO:0:3", "pv", "ac:0", ADD, -1024.0, ADD)
        ts("PJ:0:3", "pv", "ac:0", ADD, -1024.0, ADD)
        ts("PJ:3", "ac:2", n1, ADD)
        ts("PO:3", "ac:2", n1, ADD)
        ts("wt4", n2, "EG:2", MUL, "ac:1", ADD)
        ts("PJ:4:8", "PJ:0:4", 15, AND)
        cp("PF", "PJ:4:8")
        pairs = []
        for k in range(4):
            a, b, pos, lo = sub(RHk[k], 0, 64), sub(RHk[k], 64, 128), R("PO", k, k + 1), R("PF", k, k + 1)
            w = ("wt4", MUL) if k == 3 else ()
            ts(a, "IO16", 15.0, ADD, pos, GE)
            ts(b, "IO16", pos, GT)
            ts(LHk[k], "AG", lo, GE, *w)
            ts(LHk[4 + k], "AGp", lo, LT, *w)
            pairs += [(LHk[k], a), (LHk[4 + k], b)]
        mms("P6:0:64", *pairs)
        tt("lf", "P6:0:64", "SLW:0:64", ADD)
        cp("LST", "lf")
        pool = POOL(t, 0, POOLW)
        if t < RO - 1:
            utable()
            nxt = POOL(t + 1, 192, 192 + S)
            cp(sub(nxt, 0, 512), (pool, "LST:0:32"))
            act(sub(nxt, 512, 1024), (pool, "LST:32:64"), Fn.Copy)
        else:
            for k in range(3):
                act(RHk[k], "R0", Fn.Sign, scale=-1.0, bias=R("YB", k, k + 1))
            mms("P5:0:256", ("Y3", RHk[0]), ("Y1", RHk[1]), ("Y1", RHk[2]))
            act("yct", "P5:0:256", Fn.Copy, bias=0.5)
            dma("Y", "dC", T.yc[:, :], v("yct"), [R("yct")], [])
            ts("YG:0:512", (pool, "LST:0:32"), 255.0, ADD)
            act("YG:512:1024", (pool, "LST:32:64"), Fn.Copy, bias=255.0)
            dma("Y", "dY0", T.yg[:, 0:512], T.YG[:, 0:512], [R("YG", 0, 512)], [])
            dma("S", "dY1", T.yg[:, 512:1024], T.YG[:, 512:1024], [R("YG", 512, 1024)], [])
    emit()
    g.wait_ge(T.sem.lsem, 2 * RO * sent)
    for e, n in list(cnt.items()) + [(d, 16) for d in LOADS]:
        g.wait_ge(T.sem["s" + e if e in cnt else e], n)
